import numpy as np
import ml_dtypes


def mxq(x, axis, fmt="e4m3"):
    dtype, down = {"e4m3": (ml_dtypes.float8_e4m3fn, 7), "e5m2": (ml_dtypes.float8_e5m2, 14)}[fmt]
    v = np.moveaxis(np.asarray(x, np.float32).astype(ml_dtypes.bfloat16).astype(np.float64), axis, -1)
    blocks = v.reshape(v.shape[:-1] + (-1, 32))
    amax = np.abs(blocks).max(-1, keepdims=True)
    byte = np.maximum(np.where(amax > 0, np.frexp(amax)[1] - 1 + 127, 0) - down, 1)
    scale = np.exp2(byte - 127.0)
    codes = (blocks / scale).astype(np.float32).astype(dtype).astype(np.float64)
    return np.moveaxis((codes * scale).reshape(v.shape), -1, axis)


WIDE = False


def mx_kscale(k):
    if not WIDE:
        return np.ones(k)
    levels = np.array([30, -30])
    if k % 512:
        return np.exp2(np.random.permutation(np.resize(levels, k // 32))).repeat(32)
    a = np.empty((k // 512, 16))
    for p in range(k // 512):
        a[p, :8] = np.random.permutation(np.resize(levels, 8))
        for g in range(8):
            far = levels[np.abs(levels - a[p, g]) >= 10]
            a[p, g + 8] = far[np.random.randint(len(far))]
    return np.exp2(a.ravel()).repeat(32)


def f64(x):
    return np.asarray(x).astype(np.float64)


def striped(idx):
    return np.tile(idx.reshape(-1, 16).T, (8, 1)).astype(np.uint16)


def unstriped(offs):
    return offs[:16].T.reshape(-1).astype(np.int64)


E2M1 = np.array([0.0, 0.5, 1.0, 1.5, 2.0, 3.0, 4.0, 6.0, -0.0, -0.5, -1.0, -1.5, -2.0, -3.0, -4.0, -6.0])


def pack_weight(w, fmt):
    k, n = w.shape
    w = f64(np.asarray(w, np.float32).astype(ml_dtypes.bfloat16)).reshape(k // 32, 32, n)
    amax = np.abs(w).max(1)
    if fmt == "e4m3":
        byte = np.frexp(amax)[1] - 1 + 127 - 7
    elif fmt == "e5m2":
        byte = np.frexp(amax)[1] - 1 + 127 - 14
    else:
        mant, ex = np.frexp(amax / 6.0)
        byte = np.where(mant > 0.5, ex, ex - 1) + 127
    byte = np.clip(np.where(amax > 0, byte, 1), 1, 254)
    scaled = (w * np.exp2(127.0 - byte)[:, None, :]).reshape(k, n).astype(np.float32)
    by_word = np.ascontiguousarray(scaled.reshape(k // 512, 128, 4, n).transpose(0, 1, 3, 2))
    if fmt == "e4m3":
        words = by_word.astype(ml_dtypes.float8_e4m3fn).view(np.uint8)
    elif fmt == "e5m2":
        words = by_word.astype(ml_dtypes.float8_e5m2).view(np.uint8)
    else:
        c = by_word.astype(ml_dtypes.float4_e2m1fn).view(np.uint8) & 0xF
        words = (c[..., 0::2] | (c[..., 1::2] << 4)).reshape(k // 512, 128, 2 * n)
    return np.ascontiguousarray(words), np.ascontiguousarray(byte.astype(np.uint8).reshape(k // 512, 16, n))


def unpack_weight(words, scales, fmt):
    g, _, n = scales.shape
    words = np.ascontiguousarray(words).reshape(g, 128, n, -1)
    if fmt == "e4m3":
        vals = words.view(ml_dtypes.float8_e4m3fn).astype(np.float64)
    elif fmt == "e5m2":
        vals = words.view(ml_dtypes.float8_e5m2).astype(np.float64)
    else:
        nib = np.empty((g, 128, n, 4), np.uint8)
        nib[..., 0::2] = words & 0xF
        nib[..., 1::2] = words >> 4
        vals = E2M1[nib]
    vals = vals * np.repeat(np.exp2(scales.astype(np.float64) - 127.0), 8, axis=1)[..., None]
    return vals.transpose(0, 1, 3, 2).reshape(g * 512, n)


def silu(v):
    return v / (1.0 + np.exp(-np.maximum(v, -700.0)))


def d_silu(v):
    s = 1.0 / (1.0 + np.exp(-np.maximum(v, -700.0)))
    return s * (1.0 + v * (1.0 - s))


K, T, E, C, H, N = 128, 1024, 4, 512, 512, 512


def by_expert(wq, xq):
    return np.concatenate([wq[e].T @ xq[:, e * C:(e + 1) * C] for e in range(E)], axis=1)


def setup_inputs():
    n = np.random.standard_normal
    s = mx_kscale(N)[:, None]
    u = mx_kscale(H)
    first = np.random.permutation(np.repeat(np.arange(E), T // E))
    second = (first + 1 + np.random.permutation(np.repeat(np.arange(E - 1), -(-T // (E - 1)))[:T])) % E
    while np.bincount(second, minlength=E).max() != T // E:
        load = np.bincount(second, minlength=E); hi, lo = int(load.argmax()), int(load.argmin())
        t = np.flatnonzero((second == hi) & (first != lo))[0]; second[t] = lo
    slot_token = np.empty(E * C, np.int64); pos = np.empty((2, T), np.int64); fill = np.zeros(E, np.int64)
    place = np.stack([np.random.permutation(C) for _ in range(E)])
    for r, deal in enumerate((first, second)):
        for t in np.random.permutation(T):
            e = deal[t]; j = e * C + place[e, fill[e]]; fill[e] += 1; slot_token[j] = t; pos[r, t] = j
    g = np.random.uniform(0.2, 0.8, T)
    w_slot = np.empty(E * C); w_slot[pos[0]] = g; w_slot[pos[1]] = 1.0 - g
    dy = pack_weight(n((N, T)) * s, "e5m2")
    w2 = [pack_weight(m, "e2m1") for m in n((E, N, H)) / np.sqrt(N) / s[None] * u[None, None, :]]
    w1 = [pack_weight(m, "e2m1") for m in n((E, H, K)) / np.sqrt(H) / u[None, :, None]]
    w3 = [pack_weight(m, "e2m1") for m in n((E, H, K)) / np.sqrt(H) / u[None, :, None]]
    return {
        "dy_words": dy[0],
        "dy_scales": dy[1],
        "a1": n((H, E * C)).astype(np.float32),
        "a3": n((H, E * C)).astype(np.float32),
        "w2_words": np.stack([m[0] for m in w2]),
        "w2_scales": np.stack([m[1] for m in w2]),
        "w1_words": np.stack([m[0] for m in w1]),
        "w1_scales": np.stack([m[1] for m in w1]),
        "w3_words": np.stack([m[0] for m in w3]),
        "w3_scales": np.stack([m[1] for m in w3]),
        "gate": np.tile(w_slot, (H, 1)).astype(np.float32),
        "offs": striped(slot_token),
        "pos1": striped(pos[0]),
        "pos2": striped(pos[1]),
    }


def reference(dy_words, dy_scales, a1, a3, w2_words, w2_scales, w1_words, w1_scales, w3_words, w3_scales, gate, offs, pos1, pos2):
    idx = unstriped(offs)
    w2 = np.stack([unpack_weight(w2_words[e], w2_scales[e], "e2m1") for e in range(E)])
    w1 = np.stack([unpack_weight(w1_words[e], w1_scales[e], "e2m1") for e in range(E)])
    w3 = np.stack([unpack_weight(w3_words[e], w3_scales[e], "e2m1") for e in range(E)])
    gq = unpack_weight(dy_words, dy_scales, "e5m2")[:, idx]
    dh = f64(gate) * by_expert(w2, gq)
    da1 = dh * f64(a3) * d_silu(f64(a1))
    da3 = dh * silu(f64(a1))
    dx = by_expert(w1, mxq(da1, 0, "e5m2")) + by_expert(w3, mxq(da3, 0, "e5m2"))
    return dx[:, unstriped(pos1)] + dx[:, unstriped(pos2)]

@@ -1,0 +1,243 @@
+from contextlib import ExitStack
+
+import concourse.mybir as mybir
+from concourse.masks import make_identity
+
+K, T, E, C, H, N = 128, 1024, 4, 512, 512, 512
+FLOPS = 2 * E * C * (N * H + 2 * H * K)
+BYTES = T * N + T * 16 + 2 * 4 * H * E * C + E * (N * H + 2 * H * K) // 2 + E * 16 * (H + 2 * K) + 4 * E * C + 2 * 128 * 256 + 4 * K * T
+
+F32 = mybir.dt.float32
+BF16 = mybir.dt.bfloat16
+I32 = mybir.dt.int32
+U32 = mybir.dt.uint32
+U16 = mybir.dt.uint16
+U8 = mybir.dt.uint8
+E5M2X4 = mybir.dt.float8_e5m2_x4
+E2M1X4 = mybir.dt.float4_e2m1fn_x4
+ACT = mybir.ActivationFunctionType
+ALU = mybir.AluOpType
+
+P = 128
+TILES = E * C // P
+PER_EXPERT = C // P
+PIECE = 256
+
+
+def tile_moe_bdx_glu_silu_kernel(
+    tc, dy_words, dy_scales, a1, a3, w2_words, w2_scales, w1_words, w1_scales, w3_words, w3_scales,
+    gate, offs, pos1, pos2, out,
+):
+    nc = tc.nc
+    with ExitStack() as ctx:
+        keep = ctx.enter_context(tc.tile_pool(name="keep", bufs=1))
+        work = ctx.enter_context(tc.tile_pool(name="work", bufs=3))
+        psum = ctx.enter_context(tc.psum_pool(name="psum", bufs=1))
+
+        offs_sb = keep.tile([P, E * C // 16], U16, name="offs_sb")
+        pos1_sb = keep.tile([P, T // 16], U16, name="pos1_sb")
+        pos2_sb = keep.tile([P, T // 16], U16, name="pos2_sb")
+        dy_w = keep.tile([P, T], I32, name="dy_w", align_bytes=64)
+        dy_s = keep.tile([P, T], U8, name="dy_s", align_bytes=64)
+        w2_w = keep.tile([P, E * 2 * H], U8, name="w2_w", align_bytes=64)
+        w2_s = keep.tile([P, E * H], U8, name="w2_s", align_bytes=64)
+        w13_w = keep.tile([P, 2 * E * 2 * K], U8, name="w13_w", align_bytes=64)
+        w13_s = keep.tile([P, 2 * E * K], U8, name="w13_s", align_bytes=64)
+        gate_rows = keep.tile([P, P], F32, name="gate_rows")
+        half_gate = keep.tile([P, TILES], F32, name="half_gate")
+        neg_half_gate = keep.tile([P, TILES], F32, name="neg_half_gate")
+        ident = keep.tile([P, P], F32, name="ident")
+        dx = keep.tile([P, E * C], F32, name="dx")
+        a1_sb = [keep.tile([P, 4, C], F32, name="a1_sb%d" % e) for e in range(E)]
+        a3_sb = [keep.tile([P, 4, C], F32, name="a3_sb%d" % e) for e in range(E)]
+        g_w = [keep.tile([P, C], U32, name="g_w%d" % e, align_bytes=64) for e in range(E)]
+        g_s = [keep.tile([P, C], U8, name="g_s%d" % e, align_bytes=64) for e in range(E)]
+
+        for plane in (dy_s, w2_s, w13_s):
+            nc.vector.memset(plane[:].bitcast(I32), 0)
+        make_identity(nc, ident[:])
+
+        def load_scales(plane_view, scales):
+            rows = scales.rearrange("e s f c -> f (e s) c")
+            for q in range(4):
+                nc.sync.dma_start(out=plane_view[32 * q : 32 * q + 4].bitcast(I32), in_=rows[4 * q : 4 * q + 4].bitcast(I32))
+
+        def load_saved(dst, src, e):
+            nc.sync.dma_start(out=dst[e][:], in_=src[:, e * C : (e + 1) * C].rearrange("(b m) s -> m b s", m=P))
+
+        def load_w2(e0, e1):
+            nc.sync.dma_start(
+                out=w2_w[:].rearrange("p (e c) -> p e c", e=E)[:, e0:e1].bitcast(I32),
+                in_=w2_words.rearrange("e s p c -> p (e s) c")[:, e0:e1].bitcast(I32),
+            )
+
+        nc.sync.dma_start(out=dy_w[:], in_=dy_words[0].rearrange("p t d -> p (t d)").bitcast(I32))
+        nc.sync.dma_start(offs_sb[:], offs)
+        for q in range(4):
+            nc.sync.dma_start(out=dy_s[32 * q : 32 * q + 4, :].bitcast(I32), in_=dy_scales[0, 4 * q : 4 * q + 4, :].bitcast(I32))
+        load_scales(w2_s[:].rearrange("p (e c) -> p e c", e=E), w2_scales)
+        load_saved(a1_sb, a1, 0)
+        nc.sync.dma_start(out=gate_rows[:], in_=gate[0 : P // TILES, :].rearrange("r (c p) -> (r c) p", p=P))
+        load_w2(0, 1)
+        load_saved(a3_sb, a3, 0)
+        load_saved(a1_sb, a1, 1)
+        load_w2(1, E)
+        load_saved(a3_sb, a3, 1)
+        w13_w_view = w13_w[:].rearrange("p (a e c) -> p a e c", a=2, e=E)
+        w13_s_view = w13_s[:].rearrange("p (a e c) -> p a e c", a=2, e=E)
+        for a, (words, scales) in enumerate(((w1_words, w1_scales), (w3_words, w3_scales))):
+            load_scales(w13_s_view[:, a], scales)
+        for a, (words, scales) in enumerate(((w1_words, w1_scales), (w3_words, w3_scales))):
+            nc.sync.dma_start(out=w13_w_view[:, a].bitcast(I32), in_=words.rearrange("e s p c -> p (e s) c").bitcast(I32))
+        for e in range(2, E):
+            load_saved(a1_sb, a1, e)
+            load_saved(a3_sb, a3, e)
+        nc.sync.dma_start(pos1_sb[:], pos1)
+        nc.sync.dma_start(pos2_sb[:], pos2)
+
+        gate_bank = psum.tile([P, 4 * P], F32, name="gate_bank", tag="back", bufs=2)
+        nc.tensor.transpose(gate_bank[:, 0:P], gate_rows[:], ident[:])
+        nc.scalar.activation(out=half_gate[:], in_=gate_bank[:, 0:TILES], func=ACT.Copy, scale=0.5)
+        nc.scalar.activation(out=neg_half_gate[:], in_=gate_bank[:, 0:TILES], func=ACT.Copy, scale=-0.5)
+
+        def gather(e):
+            entries = offs_sb[:, e * C // 16 : (e + 1) * C // 16]
+            nc.vector.tensor_copy(g_w[e][:], dy_w[:].bitcast(U32).indirect(entries))
+            nc.vector.tensor_copy(g_s[e][:], dy_s[:].indirect(entries))
+
+        def turn(bank, src):
+            cols = bank[:].rearrange("s (u b q e) -> s b q u e", u=2, b=4, e=2)
+            for b in range(4):
+                nc.tensor.transpose(cols[:, b], src[:, b, :], ident[:])
+
+        st = {}
+
+        def front(t):
+            e, j = divmod(t, PER_EXPERT)
+            slots = slice(j * P, (j + 1) * P)
+            w = work.tile([P, 4, P], F32, name="w")
+            nc.scalar.activation(out=w[:], in_=a1_sb[e][:, :, slots], func=ACT.Silu, scale=-1.0)
+            v_t = psum.tile([P, H], F32, name="v_t", bufs=3)
+            turn(v_t, a1_sb[e][:, :, slots])
+            th = work.tile([P, H], F32, name="th")
+            nc.scalar.activation(out=th[:], in_=v_t[:], func=ACT.Tanh, scale=0.5)
+            n = work.tile([P, 4, P], F32, name="n")
+            nc.vector.scalar_tensor_tensor(out=n[:], in0=w[:], scalar=1.0, in1=a3_sb[e][:, :, slots], op0=ALU.subtract, op1=ALU.mult)
+            st[t] = {"v_t": v_t, "th": th, "n": n}
+
+        def middle(t):
+            e, j = divmod(t, PER_EXPERT)
+            slots = slice(j * P, (j + 1) * P)
+            s = psum.tile([P, H], F32, name="s", tag="s", bufs=1)
+            nc.tensor.matmul_mx(
+                out=s[:],
+                lhsT=g_w[e][:, slots].bitcast(E5M2X4),
+                lhsT_scale=g_s[e][:, slots],
+                rhs=w2_w[:, e * 2 * H : (e + 1) * 2 * H].bitcast(E2M1X4),
+                rhs_scale=w2_s[:, e * H : (e + 1) * H],
+                start=True,
+                stop=True,
+            )
+            n_t = psum.tile([P, H], F32, name="n_t", bufs=2)
+            turn(n_t, st[t]["n"][:])
+            pr = work.tile([P, H], F32, name="pr")
+            s_cols = s[:].rearrange("s (p u e) -> s u p e", u=2, e=2)
+            for u in range(2):
+                half = slice(u * H // 2, (u + 1) * H // 2)
+                nc.vector.scalar_tensor_tensor(
+                    out=pr[:, half].rearrange("s (p e) -> s p e", e=2),
+                    in0=st[t]["th"][:, half].rearrange("s (p e) -> s p e", e=2),
+                    scalar=1.0, in1=s_cols[:, u], op0=ALU.add, op1=ALU.mult,
+                )
+            st[t]["n_t"] = n_t
+            st[t]["pr"] = pr
+
+        grouped, codes, scales = {}, {}, {}
+
+        def turn_back(da, bank, e, slots, parts):
+            for a in parts:
+                words = da[:, a, :].bitcast(F32)
+                for u in range(2):
+                    nc.tensor.transpose(bank[:, (2 * a + u) * P : (2 * a + u + 1) * P], words[:, u * P : (u + 1) * P], ident[:])
+            lo, hi = min(parts), max(parts) + 1
+            nc.scalar.copy(
+                out=grouped[e][:].bitcast(F32).rearrange("p (a s u) -> p a s u", a=2, u=2)[:, lo:hi, slots, :],
+                in_=bank[:].rearrange("p (a u r) -> p a r u", a=2, u=2)[:, lo:hi],
+            )
+
+        def quantize(e, c0, c1):
+            nc.vector.quantize_mx(out=codes[e][:, c0:c1].bitcast(E5M2X4), scales=scales[e][:, c0:c1], in_=grouped[e][:, 4 * c0 : 4 * c1])
+
+        def back(t):
+            e, j = divmod(t, PER_EXPERT)
+            slots = slice(j * P, (j + 1) * P)
+            if j == 0:
+                grouped[e] = work.tile([P, 2 * C * 4], BF16, name="grouped", bufs=2, align_bytes=64)
+                codes[e] = work.tile([P, 2 * C], U32, name="codes", bufs=2, align_bytes=64)
+                scales[e] = work.tile([P, 2 * C], U8, name="scales", bufs=2, align_bytes=64)
+            da = work.tile([P, 2, H], BF16, name="da")
+            nc.vector.scalar_tensor_tensor(
+                out=da[:, 1, :], in0=st[t]["v_t"][:], scalar=half_gate[:, t : t + 1], in1=st[t]["pr"][:], op0=ALU.mult, op1=ALU.mult
+            )
+            nc.vector.scalar_tensor_tensor(
+                out=da[:, 0, :], in0=st[t]["n_t"][:], scalar=neg_half_gate[:, t : t + 1], in1=st[t]["pr"][:], op0=ALU.mult, op1=ALU.mult
+            )
+            for parts in ([(1,), (0,)] if t == TILES - 1 else [(1, 0)]):
+                bank = psum.tile([P, 4 * P], F32, name="bank", tag="back", bufs=2)
+                turn_back(da, bank, e, slots, parts)
+
+        def quantize_after(t):
+            e, j = divmod(t, PER_EXPERT)
+            if e < E - 1:
+                if j == PER_EXPERT - 1:
+                    quantize(e, 0, 2 * C)
+            elif j > 0:
+                first_slot = 0 if j == 1 else j * P
+                for a in (1, 0):
+                    quantize(e, a * C + first_slot, a * C + (j + 1) * P)
+
+        def finish(e):
+            if e < E - 1:
+                acc = psum.tile([P, C], F32, name="acc", tag="back", bufs=2)
+            else:
+                acc = psum.tile([P, C], F32, name="acc", tag="s", bufs=1)
+            for a in (1, 0):
+                nc.tensor.matmul_mx(
+                    out=acc[:],
+                    lhsT=w13_w_view[:, a, e, :].bitcast(E2M1X4),
+                    lhsT_scale=w13_s_view[:, a, e, :],
+                    rhs=codes[e][:, a * C : (a + 1) * C].bitcast(E5M2X4),
+                    rhs_scale=scales[e][:, a * C : (a + 1) * C],
+                    start=(a == 1),
+                    stop=(a == 0),
+                )
+            if e < E - 1:
+                nc.scalar.copy(out=dx[:, e * C : (e + 1) * C], in_=acc[:])
+            else:
+                nc.vector.tensor_copy(out=dx[:, e * C : (e + 1) * C], in_=acc[:])
+
+        gather(0)
+        for step in range(TILES + 3):
+            if step < TILES:
+                front(step)
+            if 0 <= step - 1 < TILES:
+                middle(step - 1)
+            if 0 <= step - 2 < TILES:
+                back(step - 2)
+            if step >= 3:
+                quantize_after(step - 3)
+            if step >= 3 and (step - 3) % PER_EXPERT == PER_EXPERT - 1:
+                finish((step - 3) // PER_EXPERT)
+            if step % PER_EXPERT == 1 and step // PER_EXPERT + 1 < E:
+                gather(step // PER_EXPERT + 1)
+
+        first = keep.tile([P, T], F32, name="first")
+        second = keep.tile([P, T], F32, name="second")
+        total = keep.tile([P, T], F32, name="total")
+        for c in range(0, T, PIECE):
+            cols = slice(c, c + PIECE)
+            entries = slice(c // 16, (c + PIECE) // 16)
+            nc.vector.tensor_copy(first[:, cols], dx[:].indirect(pos1_sb[:, entries]))
+            nc.vector.tensor_copy(second[:, cols], dx[:].indirect(pos2_sb[:, entries]))
+            nc.vector.tensor_tensor(out=total[:, cols], in0=first[:, cols], in1=second[:, cols], op=ALU.add)
+            nc.sync.dma_start(out=out[:, cols], in_=total[:, cols])

@@ -22,6 +22,7 @@ P = 128
 TILES = E * C // P
 PER_EXPERT = C // P
 PIECE = 256
+CHUNKS = [(0, 256), (256, 512), (512, 1024), (1024, 1536), (1536, 2048)]
 
 
 def tile_moe_bdx_glu_silu_kernel(
@@ -45,11 +46,10 @@ def tile_moe_bdx_glu_silu_kernel(
         w13_s = keep.tile([P, 2 * E * K], U8, name="w13_s", align_bytes=64)
         gate_rows = keep.tile([P, P], F32, name="gate_rows")
         half_gate = keep.tile([P, TILES], F32, name="half_gate")
-        neg_half_gate = keep.tile([P, TILES], F32, name="neg_half_gate")
         ident = keep.tile([P, P], F32, name="ident")
         dx = keep.tile([P, E * C], F32, name="dx")
-        a1_sb = [keep.tile([P, 4, C], F32, name="a1_sb%d" % e) for e in range(E)]
-        a3_sb = [keep.tile([P, 4, C], F32, name="a3_sb%d" % e) for e in range(E)]
+        a1_sb = [keep.tile([P, 4, hi - lo], F32, name="a1_sb%d" % lo) for lo, hi in CHUNKS]
+        a3_sb = [keep.tile([P, 4, hi - lo], F32, name="a3_sb%d" % lo) for lo, hi in CHUNKS]
         g_w = [keep.tile([P, C], U32, name="g_w%d" % e, align_bytes=64) for e in range(E)]
         g_s = [keep.tile([P, C], U8, name="g_s%d" % e, align_bytes=64) for e in range(E)]
 
@@ -62,8 +62,14 @@ def tile_moe_bdx_glu_silu_kernel(
             for q in range(4):
                 nc.sync.dma_start(out=plane_view[32 * q : 32 * q + 4].bitcast(I32), in_=rows[4 * q : 4 * q + 4].bitcast(I32))
 
-        def load_saved(dst, src, e):
-            nc.sync.dma_start(out=dst[e][:], in_=src[:, e * C : (e + 1) * C].rearrange("(b m) s -> m b s", m=P))
+        def load_saved(dst, src, c):
+            lo, hi = CHUNKS[c]
+            nc.sync.dma_start(out=dst[c][:], in_=src[:, lo:hi].rearrange("(b m) s -> m b s", m=P))
+
+        def saved(tiles, t):
+            c = max(i for i, (lo, hi) in enumerate(CHUNKS) if lo <= t * P)
+            lo = t * P - CHUNKS[c][0]
+            return tiles[c][:, :, lo : lo + P]
 
         def load_w2(e0, e1):
             nc.sync.dma_start(
@@ -77,33 +83,35 @@ def tile_moe_bdx_glu_silu_kernel(
             nc.sync.dma_start(out=dy_s[32 * q : 32 * q + 4, :].bitcast(I32), in_=dy_scales[0, 4 * q : 4 * q + 4, :].bitcast(I32))
         load_scales(w2_s[:].rearrange("p (e c) -> p e c", e=E), w2_scales)
         load_saved(a1_sb, a1, 0)
-        nc.sync.dma_start(out=gate_rows[:], in_=gate[0 : P // TILES, :].rearrange("r (c p) -> (r c) p", p=P))
-        load_w2(0, 1)
         load_saved(a3_sb, a3, 0)
+        load_w2(0, 1)
+        nc.sync.dma_start(out=gate_rows[:], in_=gate[0 : P // TILES, :].rearrange("r (c p) -> (r c) p", p=P))
         load_saved(a1_sb, a1, 1)
-        load_w2(1, E)
         load_saved(a3_sb, a3, 1)
+        load_saved(a1_sb, a1, 2)
+        load_w2(1, E)
+        load_saved(a3_sb, a3, 2)
         w13_w_view = w13_w[:].rearrange("p (a e c) -> p a e c", a=2, e=E)
         w13_s_view = w13_s[:].rearrange("p (a e c) -> p a e c", a=2, e=E)
         for a, (words, scales) in enumerate(((w1_words, w1_scales), (w3_words, w3_scales))):
             load_scales(w13_s_view[:, a], scales)
         for a, (words, scales) in enumerate(((w1_words, w1_scales), (w3_words, w3_scales))):
             nc.sync.dma_start(out=w13_w_view[:, a].bitcast(I32), in_=words.rearrange("e s p c -> p (e s) c").bitcast(I32))
-        for e in range(2, E):
-            load_saved(a1_sb, a1, e)
-            load_saved(a3_sb, a3, e)
+        for c in range(3, len(CHUNKS)):
+            load_saved(a1_sb, a1, c)
+            load_saved(a3_sb, a3, c)
         nc.sync.dma_start(pos1_sb[:], pos1)
         nc.sync.dma_start(pos2_sb[:], pos2)
 
         gate_bank = psum.tile([P, 4 * P], F32, name="gate_bank", tag="back", bufs=2)
         nc.tensor.transpose(gate_bank[:, 0:P], gate_rows[:], ident[:])
         nc.scalar.activation(out=half_gate[:], in_=gate_bank[:, 0:TILES], func=ACT.Copy, scale=0.5)
-        nc.scalar.activation(out=neg_half_gate[:], in_=gate_bank[:, 0:TILES], func=ACT.Copy, scale=-0.5)
 
-        def gather(e):
-            entries = offs_sb[:, e * C // 16 : (e + 1) * C // 16]
-            nc.vector.tensor_copy(g_w[e][:], dy_w[:].bitcast(U32).indirect(entries))
-            nc.vector.tensor_copy(g_s[e][:], dy_s[:].indirect(entries))
+        def gather_words(e):
+            nc.vector.tensor_copy(g_w[e][:], dy_w[:].bitcast(U32).indirect(offs_sb[:, e * C // 16 : (e + 1) * C // 16]))
+
+        def gather_scales(e):
+            nc.vector.tensor_copy(g_s[e][:], dy_s[:].indirect(offs_sb[:, e * C // 16 : (e + 1) * C // 16]))
 
         def turn(bank, src):
             cols = bank[:].rearrange("s (u b q e) -> s b q u e", u=2, b=4, e=2)
@@ -113,17 +121,23 @@ def tile_moe_bdx_glu_silu_kernel(
         st = {}
 
         def front(t):
-            e, j = divmod(t, PER_EXPERT)
-            slots = slice(j * P, (j + 1) * P)
-            w = work.tile([P, 4, P], F32, name="w")
-            nc.scalar.activation(out=w[:], in_=a1_sb[e][:, :, slots], func=ACT.Silu, scale=-1.0)
             v_t = psum.tile([P, H], F32, name="v_t", bufs=3)
-            turn(v_t, a1_sb[e][:, :, slots])
+            turn(v_t, saved(a1_sb, t))
             th = work.tile([P, H], F32, name="th")
             nc.scalar.activation(out=th[:], in_=v_t[:], func=ACT.Tanh, scale=0.5)
-            n = work.tile([P, 4, P], F32, name="n")
-            nc.vector.scalar_tensor_tensor(out=n[:], in0=w[:], scalar=1.0, in1=a3_sb[e][:, :, slots], op0=ALU.subtract, op1=ALU.mult)
-            st[t] = {"v_t": v_t, "th": th, "n": n}
+            st[t].update({"v_t": v_t, "th": th})
+
+        def early(t):
+            w = work.tile([P, 4, P], F32, name="w", bufs=4)
+            nc.scalar.activation(out=w[:], in_=saved(a1_sb, t), func=ACT.Silu, scale=-1.0)
+            w1 = work.tile([P, 4, P], F32, name="w1", bufs=4)
+            if t % 2 == 1:
+                nc.gpsimd.tensor_scalar(out=w1[:], in0=w[:], scalar1=-1.0, scalar2=1.0, op0=ALU.mult, op1=ALU.add)
+            else:
+                nc.scalar.activation(out=w1[:], in_=w[:], func=ACT.Copy, scale=-1.0, bias=1.0)
+            n = work.tile([P, 4, P], F32, name="n", bufs=4)
+            nc.gpsimd.tensor_tensor(out=n[:], in0=w1[:], in1=saved(a3_sb, t), op=ALU.mult)
+            st[t] = {"n": n}
 
         def middle(t):
             e, j = divmod(t, PER_EXPERT)
@@ -180,7 +194,7 @@ def tile_moe_bdx_glu_silu_kernel(
                 out=da[:, 1, :], in0=st[t]["v_t"][:], scalar=half_gate[:, t : t + 1], in1=st[t]["pr"][:], op0=ALU.mult, op1=ALU.mult
             )
             nc.vector.scalar_tensor_tensor(
-                out=da[:, 0, :], in0=st[t]["n_t"][:], scalar=neg_half_gate[:, t : t + 1], in1=st[t]["pr"][:], op0=ALU.mult, op1=ALU.mult
+                out=da[:, 0, :], in0=st[t]["n_t"][:], scalar=half_gate[:, t : t + 1], in1=st[t]["pr"][:], op0=ALU.mult, op1=ALU.mult
             )
             for parts in ([(1,), (0,)] if t == TILES - 1 else [(1, 0)]):
                 bank = psum.tile([P, 4 * P], F32, name="bank", tag="back", bufs=2)
@@ -216,10 +230,15 @@ def tile_moe_bdx_glu_silu_kernel(
             else:
                 nc.vector.tensor_copy(out=dx[:, e * C : (e + 1) * C], in_=acc[:])
 
-        gather(0)
+        gather_words(0)
+        gather_words(1)
+        gather_scales(0)
+        early(0)
         for step in range(TILES + 3):
             if step < TILES:
                 front(step)
+            if step + 1 < TILES:
+                early(step + 1)
             if 0 <= step - 1 < TILES:
                 middle(step - 1)
             if 0 <= step - 2 < TILES:
@@ -229,7 +248,9 @@ def tile_moe_bdx_glu_silu_kernel(
             if step >= 3 and (step - 3) % PER_EXPERT == PER_EXPERT - 1:
                 finish((step - 3) // PER_EXPERT)
             if step % PER_EXPERT == 1 and step // PER_EXPERT + 1 < E:
-                gather(step // PER_EXPERT + 1)
+                if step > 1:
+                    gather_words(step // PER_EXPERT + 1)
+                gather_scales(step // PER_EXPERT + 1)
 
         first = keep.tile([P, T], F32, name="first")
         second = keep.tile([P, T], F32, name="second")

@@ -22,6 +22,9 @@ P = 128
 TILES = E * C // P
 PER_EXPERT = C // P
 PIECE = 256
+GW, GS = 3, 2
+FINISH = [15, 16, 17]
+WB, NB, LEAD = 6, 8, 2
 CHUNKS = [(0, 256), (256, 512), (512, 1024), (1024, 1536), (1536, 2048)]
 
 
@@ -50,10 +53,12 @@ def tile_moe_bdx_glu_silu_kernel(
         dx = keep.tile([P, E * C], F32, name="dx")
         a1_sb = [keep.tile([P, 4, hi - lo], F32, name="a1_sb%d" % lo) for lo, hi in CHUNKS]
         a3_sb = [keep.tile([P, 4, hi - lo], F32, name="a3_sb%d" % lo) for lo, hi in CHUNKS]
-        g_w = [keep.tile([P, C], U32, name="g_w%d" % e, align_bytes=64) for e in range(E)]
-        g_s = [keep.tile([P, C], U8, name="g_s%d" % e, align_bytes=64) for e in range(E)]
+        g_w = [keep.tile([P, C], U32, name="g_w%d" % i, align_bytes=64) for i in range(GW)]
+        g_s = [keep.tile([P, C], U8, name="g_s%d" % i, align_bytes=64) for i in range(GS)]
+        sn = [psum.tile([P, H], F32, name="sn%d" % i) for i in range(3)]
 
-        for plane in (dy_s, w2_s, w13_s):
+        nc.gpsimd.memset(dy_s[:].bitcast(I32), 0)
+        for plane in (w2_s, w13_s):
             nc.vector.memset(plane[:].bitcast(I32), 0)
         make_identity(nc, ident[:])
 
@@ -77,13 +82,15 @@ def tile_moe_bdx_glu_silu_kernel(
                 in_=w2_words.rearrange("e s p c -> p (e s) c")[:, e0:e1].bitcast(I32),
             )
 
-        nc.sync.dma_start(out=dy_w[:], in_=dy_words[0].rearrange("p t d -> p (t d)").bitcast(I32))
+        w13_w_view = w13_w[:].rearrange("p (a e c) -> p a e c", a=2, e=E)
+        w13_s_view = w13_s[:].rearrange("p (a e c) -> p a e c", a=2, e=E)
         nc.sync.dma_start(offs_sb[:], offs)
         for q in range(4):
             nc.sync.dma_start(out=dy_s[32 * q : 32 * q + 4, :].bitcast(I32), in_=dy_scales[0, 4 * q : 4 * q + 4, :].bitcast(I32))
-        load_scales(w2_s[:].rearrange("p (e c) -> p e c", e=E), w2_scales)
+        nc.sync.dma_start(out=dy_w[:], in_=dy_words[0].rearrange("p t d -> p (t d)").bitcast(I32))
         load_saved(a1_sb, a1, 0)
         load_saved(a3_sb, a3, 0)
+        load_scales(w2_s[:].rearrange("p (e c) -> p e c", e=E), w2_scales)
         load_w2(0, 1)
         nc.sync.dma_start(out=gate_rows[:], in_=gate[0 : P // TILES, :].rearrange("r (c p) -> (r c) p", p=P))
         load_saved(a1_sb, a1, 1)
@@ -91,15 +98,13 @@ def tile_moe_bdx_glu_silu_kernel(
         load_saved(a1_sb, a1, 2)
         load_w2(1, E)
         load_saved(a3_sb, a3, 2)
-        w13_w_view = w13_w[:].rearrange("p (a e c) -> p a e c", a=2, e=E)
-        w13_s_view = w13_s[:].rearrange("p (a e c) -> p a e c", a=2, e=E)
-        for a, (words, scales) in enumerate(((w1_words, w1_scales), (w3_words, w3_scales))):
-            load_scales(w13_s_view[:, a], scales)
-        for a, (words, scales) in enumerate(((w1_words, w1_scales), (w3_words, w3_scales))):
-            nc.sync.dma_start(out=w13_w_view[:, a].bitcast(I32), in_=words.rearrange("e s p c -> p (e s) c").bitcast(I32))
         for c in range(3, len(CHUNKS)):
             load_saved(a1_sb, a1, c)
             load_saved(a3_sb, a3, c)
+        load_scales(w13_s_view[:, 0], w1_scales)
+        load_scales(w13_s_view[:, 1], w3_scales)
+        for a, words in enumerate((w1_words, w3_words)):
+            nc.sync.dma_start(out=w13_w_view[:, a].bitcast(I32), in_=words.rearrange("e s p c -> p (e s) c").bitcast(I32))
         nc.sync.dma_start(pos1_sb[:], pos1)
         nc.sync.dma_start(pos2_sb[:], pos2)
 
@@ -108,10 +113,10 @@ def tile_moe_bdx_glu_silu_kernel(
         nc.scalar.activation(out=half_gate[:], in_=gate_bank[:, 0:TILES], func=ACT.Copy, scale=0.5)
 
         def gather_words(e):
-            nc.vector.tensor_copy(g_w[e][:], dy_w[:].bitcast(U32).indirect(offs_sb[:, e * C // 16 : (e + 1) * C // 16]))
+            nc.vector.tensor_copy(g_w[e % GW][:], dy_w[:].bitcast(U32).indirect(offs_sb[:, e * C // 16 : (e + 1) * C // 16]))
 
         def gather_scales(e):
-            nc.vector.tensor_copy(g_s[e][:], dy_s[:].indirect(offs_sb[:, e * C // 16 : (e + 1) * C // 16]))
+            nc.vector.tensor_copy(g_s[e % GS][:], dy_s[:].indirect(offs_sb[:, e * C // 16 : (e + 1) * C // 16]))
 
         def turn(bank, src):
             cols = bank[:].rearrange("s (u b q e) -> s b q u e", u=2, b=4, e=2)
@@ -128,32 +133,30 @@ def tile_moe_bdx_glu_silu_kernel(
             st[t].update({"v_t": v_t, "th": th})
 
         def early(t):
-            w = work.tile([P, 4, P], F32, name="w", bufs=4)
+            w = work.tile([P, 4, P], F32, name="w", bufs=WB)
             nc.scalar.activation(out=w[:], in_=saved(a1_sb, t), func=ACT.Silu, scale=-1.0)
-            w1 = work.tile([P, 4, P], F32, name="w1", bufs=4)
+            w1 = work.tile([P, 4, P], F32, name="w1", bufs=WB)
             if t % 2 == 1:
                 nc.gpsimd.tensor_scalar(out=w1[:], in0=w[:], scalar1=-1.0, scalar2=1.0, op0=ALU.mult, op1=ALU.add)
             else:
                 nc.scalar.activation(out=w1[:], in_=w[:], func=ACT.Copy, scale=-1.0, bias=1.0)
-            n = work.tile([P, 4, P], F32, name="n", bufs=4)
+            n = work.tile([P, 4, P], F32, name="n", bufs=NB)
             nc.gpsimd.tensor_tensor(out=n[:], in0=w1[:], in1=saved(a3_sb, t), op=ALU.mult)
             st[t] = {"n": n}
 
         def middle(t):
             e, j = divmod(t, PER_EXPERT)
             slots = slice(j * P, (j + 1) * P)
-            s = psum.tile([P, H], F32, name="s", tag="s", bufs=1)
+            s = sn[t % 3]
             nc.tensor.matmul_mx(
                 out=s[:],
-                lhsT=g_w[e][:, slots].bitcast(E5M2X4),
-                lhsT_scale=g_s[e][:, slots],
+                lhsT=g_w[e % GW][:, slots].bitcast(E5M2X4),
+                lhsT_scale=g_s[e % GS][:, slots],
                 rhs=w2_w[:, e * 2 * H : (e + 1) * 2 * H].bitcast(E2M1X4),
                 rhs_scale=w2_s[:, e * H : (e + 1) * H],
                 start=True,
                 stop=True,
             )
-            n_t = psum.tile([P, H], F32, name="n_t", bufs=2)
-            turn(n_t, st[t]["n"][:])
             pr = work.tile([P, H], F32, name="pr")
             s_cols = s[:].rearrange("s (p u e) -> s u p e", u=2, e=2)
             for u in range(2):
@@ -163,7 +166,8 @@ def tile_moe_bdx_glu_silu_kernel(
                     in0=st[t]["th"][:, half].rearrange("s (p e) -> s p e", e=2),
                     scalar=1.0, in1=s_cols[:, u], op0=ALU.add, op1=ALU.mult,
                 )
-            st[t]["n_t"] = n_t
+            turn(s, st[t]["n"][:])
+            st[t]["n_t"] = s
             st[t]["pr"] = pr
 
         grouped, codes, scales = {}, {}, {}
@@ -182,17 +186,21 @@ def tile_moe_bdx_glu_silu_kernel(
         def quantize(e, c0, c1):
             nc.vector.quantize_mx(out=codes[e][:, c0:c1].bitcast(E5M2X4), scales=scales[e][:, c0:c1], in_=grouped[e][:, 4 * c0 : 4 * c1])
 
-        def back(t):
-            e, j = divmod(t, PER_EXPERT)
-            slots = slice(j * P, (j + 1) * P)
-            if j == 0:
-                grouped[e] = work.tile([P, 2 * C * 4], BF16, name="grouped", bufs=2, align_bytes=64)
-                codes[e] = work.tile([P, 2 * C], U32, name="codes", bufs=2, align_bytes=64)
-                scales[e] = work.tile([P, 2 * C], U8, name="scales", bufs=2, align_bytes=64)
+        def back3(t):
             da = work.tile([P, 2, H], BF16, name="da")
             nc.vector.scalar_tensor_tensor(
                 out=da[:, 1, :], in0=st[t]["v_t"][:], scalar=half_gate[:, t : t + 1], in1=st[t]["pr"][:], op0=ALU.mult, op1=ALU.mult
             )
+            st[t]["da"] = da
+
+        def back1(t):
+            e, j = divmod(t, PER_EXPERT)
+            slots = slice(j * P, (j + 1) * P)
+            if j == 0:
+                grouped[e] = work.tile([P, 2 * C * 4], BF16, name="grouped", bufs=E, align_bytes=64)
+                codes[e] = work.tile([P, 2 * C], U32, name="codes", bufs=E, align_bytes=64)
+                scales[e] = work.tile([P, 2 * C], U8, name="scales", bufs=E, align_bytes=64)
+            da = st[t]["da"]
             nc.vector.scalar_tensor_tensor(
                 out=da[:, 0, :], in0=st[t]["n_t"][:], scalar=half_gate[:, t : t + 1], in1=st[t]["pr"][:], op0=ALU.mult, op1=ALU.mult
             )
@@ -214,7 +222,7 @@ def tile_moe_bdx_glu_silu_kernel(
             if e < E - 1:
                 acc = psum.tile([P, C], F32, name="acc", tag="back", bufs=2)
             else:
-                acc = psum.tile([P, C], F32, name="acc", tag="s", bufs=1)
+                acc = sn[TILES % 3]
             for a in (1, 0):
                 nc.tensor.matmul_mx(
                     out=acc[:],
@@ -230,23 +238,28 @@ def tile_moe_bdx_glu_silu_kernel(
             else:
                 nc.vector.tensor_copy(out=dx[:, e * C : (e + 1) * C], in_=acc[:])
 
+        gather_scales(0)
         gather_words(0)
         gather_words(1)
-        gather_scales(0)
-        early(0)
+        for t in range(LEAD):
+            early(t)
         for step in range(TILES + 3):
+            if step in FINISH:
+                finish(FINISH.index(step))
             if step < TILES:
                 front(step)
-            if step + 1 < TILES:
-                early(step + 1)
+            if step + LEAD < TILES:
+                early(step + LEAD)
             if 0 <= step - 1 < TILES:
                 middle(step - 1)
             if 0 <= step - 2 < TILES:
-                back(step - 2)
+                back1(step - 2)
+            if 0 <= step - 1 < TILES:
+                back3(step - 1)
             if step >= 3:
                 quantize_after(step - 3)
-            if step >= 3 and (step - 3) % PER_EXPERT == PER_EXPERT - 1:
-                finish((step - 3) // PER_EXPERT)
+            if step == TILES + 2:
+                finish(E - 1)
             if step % PER_EXPERT == 1 and step // PER_EXPERT + 1 < E:
                 if step > 1:
                     gather_words(step // PER_EXPERT + 1)

@@ -21,11 +21,11 @@ ALU = mybir.AluOpType
 P = 128
 TILES = E * C // P
 PER_EXPERT = C // P
-PIECE = 256
-GW, GS = 3, 2
-FINISH = [15, 16, 17]
-WB, NB, LEAD = 6, 8, 2
 CHUNKS = [(0, 256), (256, 512), (512, 1024), (1024, 1536), (1536, 2048)]
+LEAD = 3
+LAG = 2
+SUM_BANKS = 5
+PIECE = 256
 
 
 def tile_moe_bdx_glu_silu_kernel(
@@ -53,13 +53,13 @@ def tile_moe_bdx_glu_silu_kernel(
         dx = keep.tile([P, E * C], F32, name="dx")
         a1_sb = [keep.tile([P, 4, hi - lo], F32, name="a1_sb%d" % lo) for lo, hi in CHUNKS]
         a3_sb = [keep.tile([P, 4, hi - lo], F32, name="a3_sb%d" % lo) for lo, hi in CHUNKS]
-        g_w = [keep.tile([P, C], U32, name="g_w%d" % i, align_bytes=64) for i in range(GW)]
-        g_s = [keep.tile([P, C], U8, name="g_s%d" % i, align_bytes=64) for i in range(GS)]
-        sn = [psum.tile([P, H], F32, name="sn%d" % i) for i in range(3)]
+        g_w = [keep.tile([P, C], U32, name="g_w%d" % i, align_bytes=64) for i in range(E)]
+        g_s = [keep.tile([P, C], U8, name="g_s%d" % i, align_bytes=64) for i in range(E)]
+        sums = [psum.tile([P, H], F32, name="sums%d" % i) for i in range(SUM_BANKS)]
 
-        nc.gpsimd.memset(dy_s[:].bitcast(I32), 0)
-        for plane in (w2_s, w13_s):
+        for plane in (dy_s, w2_s, w13_s):
             nc.vector.memset(plane[:].bitcast(I32), 0)
+        nc.gpsimd.memset(gate_rows[:], 0.0)
         make_identity(nc, ident[:])
 
         def load_scales(plane_view, scales):
@@ -69,7 +69,7 @@ def tile_moe_bdx_glu_silu_kernel(
 
         def load_saved(dst, src, c):
             lo, hi = CHUNKS[c]
-            nc.sync.dma_start(out=dst[c][:], in_=src[:, lo:hi].rearrange("(b m) s -> m b s", m=P))
+            nc.sync.dma_start(out=dst[c][:], in_=src[:, lo:hi].rearrange("(p d) s -> p d s", d=4))
 
         def saved(tiles, t):
             c = max(i for i, (lo, hi) in enumerate(CHUNKS) if lo <= t * P)
@@ -85,20 +85,17 @@ def tile_moe_bdx_glu_silu_kernel(
         w13_w_view = w13_w[:].rearrange("p (a e c) -> p a e c", a=2, e=E)
         w13_s_view = w13_s[:].rearrange("p (a e c) -> p a e c", a=2, e=E)
         nc.sync.dma_start(offs_sb[:], offs)
-        for q in range(4):
-            nc.sync.dma_start(out=dy_s[32 * q : 32 * q + 4, :].bitcast(I32), in_=dy_scales[0, 4 * q : 4 * q + 4, :].bitcast(I32))
         nc.sync.dma_start(out=dy_w[:], in_=dy_words[0].rearrange("p t d -> p (t d)").bitcast(I32))
         load_saved(a1_sb, a1, 0)
+        for q in range(4):
+            nc.sync.dma_start(out=dy_s[32 * q : 32 * q + 4, :].bitcast(I32), in_=dy_scales[0, 4 * q : 4 * q + 4, :].bitcast(I32))
+        nc.sync.dma_start(out=gate_rows[0:TILES, :], in_=gate[0].rearrange("(c p) -> c p", p=P))
         load_saved(a3_sb, a3, 0)
-        load_scales(w2_s[:].rearrange("p (e c) -> p e c", e=E), w2_scales)
-        load_w2(0, 1)
-        nc.sync.dma_start(out=gate_rows[:], in_=gate[0 : P // TILES, :].rearrange("r (c p) -> (r c) p", p=P))
         load_saved(a1_sb, a1, 1)
+        load_scales(w2_s[:].rearrange("p (e c) -> p e c", e=E), w2_scales)
+        load_w2(0, E)
         load_saved(a3_sb, a3, 1)
-        load_saved(a1_sb, a1, 2)
-        load_w2(1, E)
-        load_saved(a3_sb, a3, 2)
-        for c in range(3, len(CHUNKS)):
+        for c in range(2, len(CHUNKS)):
             load_saved(a1_sb, a1, c)
             load_saved(a3_sb, a3, c)
         load_scales(w13_s_view[:, 0], w1_scales)
@@ -108,105 +105,79 @@ def tile_moe_bdx_glu_silu_kernel(
         nc.sync.dma_start(pos1_sb[:], pos1)
         nc.sync.dma_start(pos2_sb[:], pos2)
 
-        gate_bank = psum.tile([P, 4 * P], F32, name="gate_bank", tag="back", bufs=2)
+        for e in range(E):
+            entries = offs_sb[:, e * C // 16 : (e + 1) * C // 16]
+            nc.vector.tensor_copy(g_w[e][:], dy_w[:].bitcast(U32).indirect(entries))
+            nc.vector.tensor_copy(g_s[e][:], dy_s[:].indirect(entries))
+
+        gate_bank = psum.tile([P, C], F32, name="gate_bank", tag="acc")
         nc.tensor.transpose(gate_bank[:, 0:P], gate_rows[:], ident[:])
         nc.scalar.activation(out=half_gate[:], in_=gate_bank[:, 0:TILES], func=ACT.Copy, scale=0.5)
 
-        def gather_words(e):
-            nc.vector.tensor_copy(g_w[e % GW][:], dy_w[:].bitcast(U32).indirect(offs_sb[:, e * C // 16 : (e + 1) * C // 16]))
+        gated, term = {}, {}
 
-        def gather_scales(e):
-            nc.vector.tensor_copy(g_s[e % GS][:], dy_s[:].indirect(offs_sb[:, e * C // 16 : (e + 1) * C // 16]))
-
-        def turn(bank, src):
-            cols = bank[:].rearrange("s (u b q e) -> s b q u e", u=2, b=4, e=2)
-            for b in range(4):
-                nc.tensor.transpose(cols[:, b], src[:, b, :], ident[:])
-
-        st = {}
-
-        def front(t):
-            v_t = psum.tile([P, H], F32, name="v_t", bufs=3)
-            turn(v_t, saved(a1_sb, t))
+        def ahead(t):
+            v = saved(a1_sb, t)
+            v_bank = psum.tile([P, H], F32, name="v_bank", bufs=2)
+            for d in range(4):
+                nc.tensor.transpose(v_bank[:, d * P : (d + 1) * P], v[:, d, :], ident[:])
             th = work.tile([P, H], F32, name="th")
-            nc.scalar.activation(out=th[:], in_=v_t[:], func=ACT.Tanh, scale=0.5)
-            st[t].update({"v_t": v_t, "th": th})
-
-        def early(t):
-            w = work.tile([P, 4, P], F32, name="w", bufs=WB)
-            nc.scalar.activation(out=w[:], in_=saved(a1_sb, t), func=ACT.Silu, scale=-1.0)
-            w1 = work.tile([P, 4, P], F32, name="w1", bufs=WB)
+            nc.scalar.activation(out=th[:], in_=v_bank[:], func=ACT.Tanh, scale=0.5)
+            gated[t] = work.tile([P, H], F32, name="gated", bufs=6)
+            hg = half_gate[:, t : t + 1]
+            nc.scalar.activation(out=gated[t][:], in_=th[:], func=ACT.Identity, scale=hg, bias=hg)
+            w = work.tile([P, 4, P], F32, name="w")
+            nc.scalar.activation(out=w[:], in_=v, func=ACT.Silu, scale=-1.0)
+            w1 = work.tile([P, 4, P], F32, name="w1", bufs=4)
             if t % 2 == 1:
                 nc.gpsimd.tensor_scalar(out=w1[:], in0=w[:], scalar1=-1.0, scalar2=1.0, op0=ALU.mult, op1=ALU.add)
             else:
                 nc.scalar.activation(out=w1[:], in_=w[:], func=ACT.Copy, scale=-1.0, bias=1.0)
-            n = work.tile([P, 4, P], F32, name="n", bufs=NB)
-            nc.gpsimd.tensor_tensor(out=n[:], in0=w1[:], in1=saved(a3_sb, t), op=ALU.mult)
-            st[t] = {"n": n}
+            term[t] = work.tile([P, 4, P], F32, name="term", bufs=8)
+            nc.gpsimd.tensor_tensor(out=term[t][:], in0=w1[:], in1=saved(a3_sb, t), op=ALU.mult)
 
-        def middle(t):
+        def first_product(t):
             e, j = divmod(t, PER_EXPERT)
             slots = slice(j * P, (j + 1) * P)
-            s = sn[t % 3]
             nc.tensor.matmul_mx(
-                out=s[:],
-                lhsT=g_w[e % GW][:, slots].bitcast(E5M2X4),
-                lhsT_scale=g_s[e % GS][:, slots],
+                out=sums[t % SUM_BANKS][:],
+                lhsT=g_w[e][:, slots].bitcast(E5M2X4),
+                lhsT_scale=g_s[e][:, slots],
                 rhs=w2_w[:, e * 2 * H : (e + 1) * 2 * H].bitcast(E2M1X4),
                 rhs_scale=w2_s[:, e * H : (e + 1) * H],
                 start=True,
                 stop=True,
             )
-            pr = work.tile([P, H], F32, name="pr")
-            s_cols = s[:].rearrange("s (p u e) -> s u p e", u=2, e=2)
-            for u in range(2):
-                half = slice(u * H // 2, (u + 1) * H // 2)
-                nc.vector.scalar_tensor_tensor(
-                    out=pr[:, half].rearrange("s (p e) -> s p e", e=2),
-                    in0=st[t]["th"][:, half].rearrange("s (p e) -> s p e", e=2),
-                    scalar=1.0, in1=s_cols[:, u], op0=ALU.add, op1=ALU.mult,
-                )
-            turn(s, st[t]["n"][:])
-            st[t]["n_t"] = s
-            st[t]["pr"] = pr
+
+        def common(t):
+            bank = sums[t % SUM_BANKS]
+            pr = work.tile([P, 4, P], F32, name="pr")
+            nc.vector.tensor_tensor(
+                out=pr[:], in0=bank[:].rearrange("s (p d) -> s d p", d=4), in1=gated[t][:].rearrange("s (d p) -> s d p", d=4), op=ALU.mult
+            )
+            for d in range(4):
+                nc.tensor.transpose(bank[:, d * P : (d + 1) * P], pr[:, d, :], ident[:])
 
         grouped, codes, scales = {}, {}, {}
 
-        def turn_back(da, bank, e, slots, parts):
-            for a in parts:
-                words = da[:, a, :].bitcast(F32)
-                for u in range(2):
-                    nc.tensor.transpose(bank[:, (2 * a + u) * P : (2 * a + u + 1) * P], words[:, u * P : (u + 1) * P], ident[:])
-            lo, hi = min(parts), max(parts) + 1
-            nc.scalar.copy(
-                out=grouped[e][:].bitcast(F32).rearrange("p (a s u) -> p a s u", a=2, u=2)[:, lo:hi, slots, :],
-                in_=bank[:].rearrange("p (a u r) -> p a r u", a=2, u=2)[:, lo:hi],
-            )
-
-        def quantize(e, c0, c1):
-            nc.vector.quantize_mx(out=codes[e][:, c0:c1].bitcast(E5M2X4), scales=scales[e][:, c0:c1], in_=grouped[e][:, 4 * c0 : 4 * c1])
-
-        def back3(t):
-            da = work.tile([P, 2, H], BF16, name="da")
-            nc.vector.scalar_tensor_tensor(
-                out=da[:, 1, :], in0=st[t]["v_t"][:], scalar=half_gate[:, t : t + 1], in1=st[t]["pr"][:], op0=ALU.mult, op1=ALU.mult
-            )
-            st[t]["da"] = da
-
-        def back1(t):
+        def last_products(t):
             e, j = divmod(t, PER_EXPERT)
-            slots = slice(j * P, (j + 1) * P)
             if j == 0:
                 grouped[e] = work.tile([P, 2 * C * 4], BF16, name="grouped", bufs=E, align_bytes=64)
                 codes[e] = work.tile([P, 2 * C], U32, name="codes", bufs=E, align_bytes=64)
                 scales[e] = work.tile([P, 2 * C], U8, name="scales", bufs=E, align_bytes=64)
-            da = st[t]["da"]
-            nc.vector.scalar_tensor_tensor(
-                out=da[:, 0, :], in0=st[t]["n_t"][:], scalar=half_gate[:, t : t + 1], in1=st[t]["pr"][:], op0=ALU.mult, op1=ALU.mult
-            )
-            for parts in ([(1,), (0,)] if t == TILES - 1 else [(1, 0)]):
-                bank = psum.tile([P, 4 * P], F32, name="bank", tag="back", bufs=2)
-                turn_back(da, bank, e, slots, parts)
+            turned = sums[t % SUM_BANKS][:].rearrange("p (d c i) -> p c d i", d=4, i=2)
+            for a, factor in ((1, saved(a1_sb, t)), (0, term[t][:])):
+                lo = 4 * (a * C + j * P)
+                nc.vector.tensor_tensor(
+                    out=grouped[e][:, lo : lo + 4 * P].rearrange("p (c i d) -> p c d i", d=4, i=2),
+                    in0=turned,
+                    in1=factor.rearrange("p d (c i) -> p c d i", i=2),
+                    op=ALU.mult,
+                )
+
+        def quantize(e, c0, c1):
+            nc.vector.quantize_mx(out=codes[e][:, c0:c1].bitcast(E5M2X4), scales=scales[e][:, c0:c1], in_=grouped[e][:, 4 * c0 : 4 * c1])
 
         def quantize_after(t):
             e, j = divmod(t, PER_EXPERT)
@@ -219,10 +190,7 @@ def tile_moe_bdx_glu_silu_kernel(
                     quantize(e, a * C + first_slot, a * C + (j + 1) * P)
 
         def finish(e):
-            if e < E - 1:
-                acc = psum.tile([P, C], F32, name="acc", tag="back", bufs=2)
-            else:
-                acc = sn[TILES % 3]
+            acc = psum.tile([P, C], F32, name="acc", tag="acc")
             for a in (1, 0):
                 nc.tensor.matmul_mx(
                     out=acc[:],
@@ -238,40 +206,27 @@ def tile_moe_bdx_glu_silu_kernel(
             else:
                 nc.vector.tensor_copy(out=dx[:, e * C : (e + 1) * C], in_=acc[:])
 
-        gather_scales(0)
-        gather_words(0)
-        gather_words(1)
-        for t in range(LEAD):
-            early(t)
-        for step in range(TILES + 3):
-            if step in FINISH:
-                finish(FINISH.index(step))
-            if step < TILES:
-                front(step)
+        for step in range(-LEAD, TILES + LAG + 1):
             if step + LEAD < TILES:
-                early(step + LEAD)
-            if 0 <= step - 1 < TILES:
-                middle(step - 1)
-            if 0 <= step - 2 < TILES:
-                back1(step - 2)
-            if 0 <= step - 1 < TILES:
-                back3(step - 1)
-            if step >= 3:
-                quantize_after(step - 3)
-            if step == TILES + 2:
-                finish(E - 1)
-            if step % PER_EXPERT == 1 and step // PER_EXPERT + 1 < E:
-                if step > 1:
-                    gather_words(step // PER_EXPERT + 1)
-                gather_scales(step // PER_EXPERT + 1)
+                ahead(step + LEAD)
+            if 0 <= step + 1 < TILES:
+                first_product(step + 1)
+            if 0 <= step < TILES:
+                common(step)
+            if 0 <= step - LAG < TILES:
+                last_products(step - LAG)
+            done = step - LAG - 1
+            if done >= 0:
+                quantize_after(done)
+            if done >= PER_EXPERT and done % PER_EXPERT == PER_EXPERT - 2:
+                finish(done // PER_EXPERT - 1)
+        finish(E - 1)
 
         first = keep.tile([P, T], F32, name="first")
-        second = keep.tile([P, T], F32, name="second")
         total = keep.tile([P, T], F32, name="total")
+        for c in range(0, T, 2 * PIECE):
+            nc.vector.tensor_copy(first[:, c : c + 2 * PIECE], dx[:].indirect(pos1_sb[:, c // 16 : (c + 2 * PIECE) // 16]))
         for c in range(0, T, PIECE):
             cols = slice(c, c + PIECE)
-            entries = slice(c // 16, (c + PIECE) // 16)
-            nc.vector.tensor_copy(first[:, cols], dx[:].indirect(pos1_sb[:, entries]))
-            nc.vector.tensor_copy(second[:, cols], dx[:].indirect(pos2_sb[:, entries]))
-            nc.vector.tensor_tensor(out=total[:, cols], in0=first[:, cols], in1=second[:, cols], op=ALU.add)
+            nc.vector.tensor_tensor(total[:, cols], dx[:].indirect(pos2_sb[:, c // 16 : (c + PIECE) // 16]), first[:, cols], ALU.add)
             nc.sync.dma_start(out=out[:, cols], in_=total[:, cols])

@@ -41,7 +41,7 @@ def tile_moe_bdx_glu_silu_kernel(
         offs_sb = keep.tile([P, E * C // 16], U16, name="offs_sb")
         pos1_sb = keep.tile([P, T // 16], U16, name="pos1_sb")
         pos2_sb = keep.tile([P, T // 16], U16, name="pos2_sb")
-        dy_w = keep.tile([P, T], I32, name="dy_w", align_bytes=64)
+        dy_w = keep.tile([P, T], I32, name="dy_w", tag="early", align_bytes=64)
         dy_s = keep.tile([P, T], U8, name="dy_s", align_bytes=64)
         w2_w = keep.tile([P, E * 2 * H], U8, name="w2_w", align_bytes=64)
         w2_s = keep.tile([P, E * H], U8, name="w2_s", align_bytes=64)
@@ -57,7 +57,8 @@ def tile_moe_bdx_glu_silu_kernel(
         g_s = [keep.tile([P, C], U8, name="g_s%d" % i, align_bytes=64) for i in range(E)]
         sums = [psum.tile([P, H], F32, name="sums%d" % i) for i in range(SUM_BANKS)]
 
-        for plane in (dy_s, w2_s, w13_s):
+        nc.gpsimd.memset(dy_s[:].bitcast(I32), 0)
+        for plane in (w2_s, w13_s):
             nc.vector.memset(plane[:].bitcast(I32), 0)
         nc.gpsimd.memset(gate_rows[:], 0.0)
         make_identity(nc, ident[:])
@@ -85,10 +86,10 @@ def tile_moe_bdx_glu_silu_kernel(
         w13_w_view = w13_w[:].rearrange("p (a e c) -> p a e c", a=2, e=E)
         w13_s_view = w13_s[:].rearrange("p (a e c) -> p a e c", a=2, e=E)
         nc.sync.dma_start(offs_sb[:], offs)
-        nc.sync.dma_start(out=dy_w[:], in_=dy_words[0].rearrange("p t d -> p (t d)").bitcast(I32))
-        load_saved(a1_sb, a1, 0)
         for q in range(4):
             nc.sync.dma_start(out=dy_s[32 * q : 32 * q + 4, :].bitcast(I32), in_=dy_scales[0, 4 * q : 4 * q + 4, :].bitcast(I32))
+        load_saved(a1_sb, a1, 0)
+        nc.sync.dma_start(out=dy_w[:], in_=dy_words[0].rearrange("p t d -> p (t d)").bitcast(I32))
         nc.sync.dma_start(out=gate_rows[0:TILES, :], in_=gate[0].rearrange("(c p) -> c p", p=P))
         load_saved(a3_sb, a3, 0)
         load_saved(a1_sb, a1, 1)
@@ -106,9 +107,9 @@ def tile_moe_bdx_glu_silu_kernel(
         nc.sync.dma_start(pos2_sb[:], pos2)
 
         for e in range(E):
-            entries = offs_sb[:, e * C // 16 : (e + 1) * C // 16]
-            nc.vector.tensor_copy(g_w[e][:], dy_w[:].bitcast(U32).indirect(entries))
-            nc.vector.tensor_copy(g_s[e][:], dy_s[:].indirect(entries))
+            nc.vector.tensor_copy(g_s[e][:], dy_s[:].indirect(offs_sb[:, e * C // 16 : (e + 1) * C // 16]))
+        for e in range(E):
+            nc.vector.tensor_copy(g_w[e][:], dy_w[:].bitcast(U32).indirect(offs_sb[:, e * C // 16 : (e + 1) * C // 16]))
 
         gate_bank = psum.tile([P, C], F32, name="gate_bank", tag="acc")
         nc.tensor.transpose(gate_bank[:, 0:P], gate_rows[:], ident[:])
@@ -126,14 +127,17 @@ def tile_moe_bdx_glu_silu_kernel(
             gated[t] = work.tile([P, H], F32, name="gated", bufs=6)
             hg = half_gate[:, t : t + 1]
             nc.scalar.activation(out=gated[t][:], in_=th[:], func=ACT.Identity, scale=hg, bias=hg)
-            w = work.tile([P, 4, P], F32, name="w")
+            w = work.tile([P, 4, P], F32, name="w", bufs=6)
             nc.scalar.activation(out=w[:], in_=v, func=ACT.Silu, scale=-1.0)
-            w1 = work.tile([P, 4, P], F32, name="w1", bufs=4)
-            if t % 2 == 1:
+            w1 = work.tile([P, 4, P], F32, name="w1", bufs=6)
+            if t % 2 == 0 and t > 0:
                 nc.gpsimd.tensor_scalar(out=w1[:], in0=w[:], scalar1=-1.0, scalar2=1.0, op0=ALU.mult, op1=ALU.add)
             else:
                 nc.scalar.activation(out=w1[:], in_=w[:], func=ACT.Copy, scale=-1.0, bias=1.0)
-            term[t] = work.tile([P, 4, P], F32, name="term", bufs=8)
+            if t == 0:
+                term[t] = keep.tile([P, 4, P], F32, name="term0", tag="early", align_bytes=64)
+            else:
+                term[t] = work.tile([P, 4, P], F32, name="term", bufs=8)
             nc.gpsimd.tensor_tensor(out=term[t][:], in0=w1[:], in1=saved(a3_sb, t), op=ALU.mult)
 
         def first_product(t):

@@ -21,11 +21,18 @@ ALU = mybir.AluOpType
 P = 128
 TILES = E * C // P
 PER_EXPERT = C // P
-CHUNKS = [(0, 256), (256, 512), (512, 1024), (1024, 1536), (1536, 2048)]
-LEAD = 3
+A1_CHUNKS = [(0, 256), (256, 512), (512, 1024), (1024, 1536), (1536, 2048)]
+A3_CHUNKS = [(0, 256), (256, 512), (512, 1024), (1024, 1536), (1536, 2048)]
 LAG = 2
 SUM_BANKS = 5
+TURN_BANKS = 2
+TH_LEAD = 3
+GATED_LEAD = 3
+TERM_LEAD = 1
+NEG_LEAD = 2
+QUANTIZE_AT = (6, 10, 14)
 PIECE = 256
+STORES = [(0, 384), (384, 704), (704, 896), (896, 1024)]
 
 
 def tile_moe_bdx_glu_silu_kernel(
@@ -41,21 +48,22 @@ def tile_moe_bdx_glu_silu_kernel(
         offs_sb = keep.tile([P, E * C // 16], U16, name="offs_sb")
         pos1_sb = keep.tile([P, T // 16], U16, name="pos1_sb")
         pos2_sb = keep.tile([P, T // 16], U16, name="pos2_sb")
-        dy_w = keep.tile([P, T], I32, name="dy_w", tag="early", align_bytes=64)
+        dy_w = keep.tile([P, T], I32, name="dy_w", align_bytes=64)
         dy_s = keep.tile([P, T], U8, name="dy_s", align_bytes=64)
         w2_w = keep.tile([P, E * 2 * H], U8, name="w2_w", align_bytes=64)
         w2_s = keep.tile([P, E * H], U8, name="w2_s", align_bytes=64)
         w13_w = keep.tile([P, 2 * E * 2 * K], U8, name="w13_w", align_bytes=64)
         w13_s = keep.tile([P, 2 * E * K], U8, name="w13_s", align_bytes=64)
         gate_rows = keep.tile([P, P], F32, name="gate_rows")
-        half_gate = keep.tile([P, TILES], F32, name="half_gate")
+        gate_cols = keep.tile([P, TILES], F32, name="gate_cols")
         ident = keep.tile([P, P], F32, name="ident")
         dx = keep.tile([P, E * C], F32, name="dx")
-        a1_sb = [keep.tile([P, 4, hi - lo], F32, name="a1_sb%d" % lo) for lo, hi in CHUNKS]
-        a3_sb = [keep.tile([P, 4, hi - lo], F32, name="a3_sb%d" % lo) for lo, hi in CHUNKS]
+        a1_sb = [keep.tile([P, 4, hi - lo], F32, name="a1_sb%d" % lo) for lo, hi in A1_CHUNKS]
+        a3_sb = [keep.tile([P, 4, hi - lo], F32, name="a3_sb%d" % lo) for lo, hi in A3_CHUNKS]
         g_w = [keep.tile([P, C], U32, name="g_w%d" % i, align_bytes=64) for i in range(E)]
         g_s = [keep.tile([P, C], U8, name="g_s%d" % i, align_bytes=64) for i in range(E)]
         sums = [psum.tile([P, H], F32, name="sums%d" % i) for i in range(SUM_BANKS)]
+        turns = [psum.tile([P, H], F32, name="turns%d" % i) for i in range(TURN_BANKS)]
 
         nc.gpsimd.memset(dy_s[:].bitcast(I32), 0)
         for plane in (w2_s, w13_s):
@@ -68,13 +76,13 @@ def tile_moe_bdx_glu_silu_kernel(
             for q in range(4):
                 nc.sync.dma_start(out=plane_view[32 * q : 32 * q + 4].bitcast(I32), in_=rows[4 * q : 4 * q + 4].bitcast(I32))
 
-        def load_saved(dst, src, c):
-            lo, hi = CHUNKS[c]
+        def load_saved(dst, src, chunks, c):
+            lo, hi = chunks[c]
             nc.sync.dma_start(out=dst[c][:], in_=src[:, lo:hi].rearrange("(p d) s -> p d s", d=4))
 
-        def saved(tiles, t):
-            c = max(i for i, (lo, hi) in enumerate(CHUNKS) if lo <= t * P)
-            lo = t * P - CHUNKS[c][0]
+        def saved(tiles, chunks, t):
+            c = max(i for i, (lo, hi) in enumerate(chunks) if lo <= t * P)
+            lo = t * P - chunks[c][0]
             return tiles[c][:, :, lo : lo + P]
 
         def load_w2(e0, e1):
@@ -88,17 +96,20 @@ def tile_moe_bdx_glu_silu_kernel(
         nc.sync.dma_start(offs_sb[:], offs)
         for q in range(4):
             nc.sync.dma_start(out=dy_s[32 * q : 32 * q + 4, :].bitcast(I32), in_=dy_scales[0, 4 * q : 4 * q + 4, :].bitcast(I32))
-        load_saved(a1_sb, a1, 0)
+        load_saved(a1_sb, a1, A1_CHUNKS, 0)
         nc.sync.dma_start(out=dy_w[:], in_=dy_words[0].rearrange("p t d -> p (t d)").bitcast(I32))
         nc.sync.dma_start(out=gate_rows[0:TILES, :], in_=gate[0].rearrange("(c p) -> c p", p=P))
-        load_saved(a3_sb, a3, 0)
-        load_saved(a1_sb, a1, 1)
+        load_saved(a3_sb, a3, A3_CHUNKS, 0)
+        load_saved(a1_sb, a1, A1_CHUNKS, 1)
         load_scales(w2_s[:].rearrange("p (e c) -> p e c", e=E), w2_scales)
-        load_w2(0, E)
-        load_saved(a3_sb, a3, 1)
-        for c in range(2, len(CHUNKS)):
-            load_saved(a1_sb, a1, c)
-            load_saved(a3_sb, a3, c)
+        load_w2(0, 4)
+        load_saved(a3_sb, a3, A3_CHUNKS, 1)
+        load_saved(a1_sb, a1, A1_CHUNKS, 2)
+        load_saved(a3_sb, a3, A3_CHUNKS, 2)
+        load_saved(a1_sb, a1, A1_CHUNKS, 3)
+        load_saved(a3_sb, a3, A3_CHUNKS, 3)
+        load_saved(a1_sb, a1, A1_CHUNKS, 4)
+        load_saved(a3_sb, a3, A3_CHUNKS, 4)
         load_scales(w13_s_view[:, 0], w1_scales)
         load_scales(w13_s_view[:, 1], w3_scales)
         for a, words in enumerate((w1_words, w3_words)):
@@ -108,43 +119,54 @@ def tile_moe_bdx_glu_silu_kernel(
 
         for e in range(E):
             nc.vector.tensor_copy(g_s[e][:], dy_s[:].indirect(offs_sb[:, e * C // 16 : (e + 1) * C // 16]))
-        for e in range(E):
             nc.vector.tensor_copy(g_w[e][:], dy_w[:].bitcast(U32).indirect(offs_sb[:, e * C // 16 : (e + 1) * C // 16]))
 
-        gate_bank = psum.tile([P, C], F32, name="gate_bank", tag="acc")
-        nc.tensor.transpose(gate_bank[:, 0:P], gate_rows[:], ident[:])
-        nc.scalar.activation(out=half_gate[:], in_=gate_bank[:, 0:TILES], func=ACT.Copy, scale=0.5)
+        spare = psum.tile([P, C], F32, name="spare")
+        nc.tensor.transpose(spare[:, 0:P], gate_rows[:], ident[:])
+        nc.scalar.activation(out=gate_cols[:], in_=spare[:, 0:TILES], func=ACT.Copy, scale=0.5)
 
-        gated, term = {}, {}
+        th, gated, rest, term = {}, {}, {}, {}
 
-        def ahead(t):
-            v = saved(a1_sb, t)
-            v_bank = psum.tile([P, H], F32, name="v_bank", bufs=2)
+        def make_th(t):
+            bank = turns[t % TURN_BANKS]
+            v = saved(a1_sb, A1_CHUNKS, t)
             for d in range(4):
-                nc.tensor.transpose(v_bank[:, d * P : (d + 1) * P], v[:, d, :], ident[:])
-            th = work.tile([P, H], F32, name="th")
-            nc.scalar.activation(out=th[:], in_=v_bank[:], func=ACT.Tanh, scale=0.5)
+                nc.tensor.transpose(bank[:, d * P : (d + 1) * P], v[:, d, :], ident[:])
+            th[t] = work.tile([P, H], F32, name="th", bufs=4)
+            nc.scalar.activation(out=th[t][:], in_=bank[:], func=ACT.Tanh, scale=0.5)
+
+        def make_gated(t):
             gated[t] = work.tile([P, H], F32, name="gated", bufs=6)
-            hg = half_gate[:, t : t + 1]
-            nc.scalar.activation(out=gated[t][:], in_=th[:], func=ACT.Identity, scale=hg, bias=hg)
-            w = work.tile([P, 4, P], F32, name="w", bufs=6)
-            nc.scalar.activation(out=w[:], in_=v, func=ACT.Silu, scale=-1.0)
-            w1 = work.tile([P, 4, P], F32, name="w1", bufs=6)
-            if t % 2 == 0 and t > 0:
-                nc.gpsimd.tensor_scalar(out=w1[:], in0=w[:], scalar1=-1.0, scalar2=1.0, op0=ALU.mult, op1=ALU.add)
+            hg = gate_cols[:, t : t + 1]
+            nc.scalar.activation(out=gated[t][:], in_=th[t][:], func=ACT.Identity, scale=hg, bias=hg)
+
+        def on_gpsimd(t):
+            return t in (5, 7, 9, 11, 13)
+
+        def make_neg(t):
+            neg = work.tile([P, 4, P], F32, name="neg", bufs=4)
+            nc.scalar.activation(out=neg[:], in_=saved(a1_sb, A1_CHUNKS, t), func=ACT.Silu, scale=-1.0)
+            if on_gpsimd(t):
+                rest[t] = neg
             else:
-                nc.scalar.activation(out=w1[:], in_=w[:], func=ACT.Copy, scale=-1.0, bias=1.0)
-            if t == 0:
-                term[t] = keep.tile([P, 4, P], F32, name="term0", tag="early", align_bytes=64)
-            else:
-                term[t] = work.tile([P, 4, P], F32, name="term", bufs=8)
-            nc.gpsimd.tensor_tensor(out=term[t][:], in0=w1[:], in1=saved(a3_sb, t), op=ALU.mult)
+                rest[t] = work.tile([P, 4, P], F32, name="rest", bufs=4)
+                nc.scalar.activation(out=rest[t][:], in_=neg[:], func=ACT.Copy, scale=-1.0, bias=1.0)
+
+        def make_term(t):
+            term[t] = work.tile([P, 4, P], F32, name="term", bufs=6)
+            if on_gpsimd(t):
+                nc.gpsimd.tensor_scalar(out=term[t][:], in0=rest[t][:], scalar1=-1.0, scalar2=1.0, op0=ALU.mult, op1=ALU.add)
+                rest[t] = term[t]
+            nc.gpsimd.tensor_tensor(out=term[t][:], in0=rest[t][:], in1=saved(a3_sb, A3_CHUNKS, t), op=ALU.mult)
+
+        def sum_bank(t):
+            return sums[t % SUM_BANKS]
 
         def first_product(t):
             e, j = divmod(t, PER_EXPERT)
             slots = slice(j * P, (j + 1) * P)
             nc.tensor.matmul_mx(
-                out=sums[t % SUM_BANKS][:],
+                out=sum_bank(t)[:],
                 lhsT=g_w[e][:, slots].bitcast(E5M2X4),
                 lhsT_scale=g_s[e][:, slots],
                 rhs=w2_w[:, e * 2 * H : (e + 1) * 2 * H].bitcast(E2M1X4),
@@ -154,8 +176,8 @@ def tile_moe_bdx_glu_silu_kernel(
             )
 
         def common(t):
-            bank = sums[t % SUM_BANKS]
-            pr = work.tile([P, 4, P], F32, name="pr")
+            bank = sum_bank(t)
+            pr = work.tile([P, 4, P], F32, name="pr", bufs=3)
             nc.vector.tensor_tensor(
                 out=pr[:], in0=bank[:].rearrange("s (p d) -> s d p", d=4), in1=gated[t][:].rearrange("s (d p) -> s d p", d=4), op=ALU.mult
             )
@@ -164,37 +186,27 @@ def tile_moe_bdx_glu_silu_kernel(
 
         grouped, codes, scales = {}, {}, {}
 
-        def last_products(t):
+        def last_product(t, a):
             e, j = divmod(t, PER_EXPERT)
-            if j == 0:
+            if e not in grouped:
                 grouped[e] = work.tile([P, 2 * C * 4], BF16, name="grouped", bufs=E, align_bytes=64)
                 codes[e] = work.tile([P, 2 * C], U32, name="codes", bufs=E, align_bytes=64)
                 scales[e] = work.tile([P, 2 * C], U8, name="scales", bufs=E, align_bytes=64)
-            turned = sums[t % SUM_BANKS][:].rearrange("p (d c i) -> p c d i", d=4, i=2)
-            for a, factor in ((1, saved(a1_sb, t)), (0, term[t][:])):
-                lo = 4 * (a * C + j * P)
-                nc.vector.tensor_tensor(
-                    out=grouped[e][:, lo : lo + 4 * P].rearrange("p (c i d) -> p c d i", d=4, i=2),
-                    in0=turned,
-                    in1=factor.rearrange("p d (c i) -> p c d i", i=2),
-                    op=ALU.mult,
-                )
+            turned = sum_bank(t)[:].rearrange("p (d c i) -> p c d i", d=4, i=2)
+            factor = saved(a1_sb, A1_CHUNKS, t) if a == 1 else term[t][:]
+            lo = 4 * (a * C + j * P)
+            nc.vector.tensor_tensor(
+                out=grouped[e][:, lo : lo + 4 * P].rearrange("p (c i d) -> p c d i", d=4, i=2),
+                in0=turned,
+                in1=factor.rearrange("p d (c i) -> p c d i", i=2),
+                op=ALU.mult,
+            )
 
         def quantize(e, c0, c1):
             nc.vector.quantize_mx(out=codes[e][:, c0:c1].bitcast(E5M2X4), scales=scales[e][:, c0:c1], in_=grouped[e][:, 4 * c0 : 4 * c1])
 
-        def quantize_after(t):
-            e, j = divmod(t, PER_EXPERT)
-            if e < E - 1:
-                if j == PER_EXPERT - 1:
-                    quantize(e, 0, 2 * C)
-            elif j > 0:
-                first_slot = 0 if j == 1 else j * P
-                for a in (1, 0):
-                    quantize(e, a * C + first_slot, a * C + (j + 1) * P)
-
         def finish(e):
-            acc = psum.tile([P, C], F32, name="acc", tag="acc")
+            acc = (spare, turns[0], turns[1], spare)[e]
             for a in (1, 0):
                 nc.tensor.matmul_mx(
                     out=acc[:],
@@ -210,27 +222,42 @@ def tile_moe_bdx_glu_silu_kernel(
             else:
                 nc.vector.tensor_copy(out=dx[:, e * C : (e + 1) * C], in_=acc[:])
 
-        for step in range(-LEAD, TILES + LAG + 1):
-            if step + LEAD < TILES:
-                ahead(step + LEAD)
+        for step in range(-4, TILES + LAG):
+            if 0 <= step + TH_LEAD < TILES:
+                make_th(step + TH_LEAD)
+            if 0 <= step + GATED_LEAD < TILES:
+                make_gated(step + GATED_LEAD)
+            if 0 <= step + NEG_LEAD < TILES:
+                make_neg(step + NEG_LEAD)
+            if 0 <= step + TERM_LEAD < TILES:
+                make_term(step + TERM_LEAD)
             if 0 <= step + 1 < TILES:
                 first_product(step + 1)
             if 0 <= step < TILES:
                 common(step)
-            if 0 <= step - LAG < TILES:
-                last_products(step - LAG)
-            done = step - LAG - 1
-            if done >= 0:
-                quantize_after(done)
-            if done >= PER_EXPERT and done % PER_EXPERT == PER_EXPERT - 2:
-                finish(done // PER_EXPERT - 1)
-        finish(E - 1)
+            if 0 <= step - LAG < TILES - 2:
+                last_product(step - LAG, 1)
+                last_product(step - LAG, 0)
+            if step in QUANTIZE_AT:
+                quantize(QUANTIZE_AT.index(step), 0, 2 * C)
+        last = E - 1
+        last_product(TILES - 2, 1)
+        last_product(TILES - 2, 0)
+        for a in (1, 0):
+            quantize(last, a * C, a * C + 2 * P)
+        last_product(TILES - 1, 1)
+        last_product(TILES - 1, 0)
+        quantize(last, C + 2 * P, 2 * C)
+        quantize(last, 2 * P, 3 * P)
+        quantize(last, 3 * P, C)
+        for e in range(E):
+            finish(e)
 
         first = keep.tile([P, T], F32, name="first")
         total = keep.tile([P, T], F32, name="total")
         for c in range(0, T, 2 * PIECE):
             nc.vector.tensor_copy(first[:, c : c + 2 * PIECE], dx[:].indirect(pos1_sb[:, c // 16 : (c + 2 * PIECE) // 16]))
-        for c in range(0, T, PIECE):
-            cols = slice(c, c + PIECE)
-            nc.vector.tensor_tensor(total[:, cols], dx[:].indirect(pos2_sb[:, c // 16 : (c + PIECE) // 16]), first[:, cols], ALU.add)
+        for lo, hi in STORES:
+            cols = slice(lo, hi)
+            nc.vector.tensor_tensor(total[:, cols], dx[:].indirect(pos2_sb[:, lo // 16 : hi // 16]), first[:, cols], ALU.add)
             nc.sync.dma_start(out=out[:, cols], in_=total[:, cols])

@@ -19,19 +19,25 @@ ACT = mybir.ActivationFunctionType
 ALU = mybir.AluOpType
 
 P = 128
+PACK = 4
 TILES = E * C // P
 PER_EXPERT = C // P
-A1_CHUNKS = [(0, 256), (256, 512), (512, 1024), (1024, 1536), (1536, 2048)]
-A3_CHUNKS = [(0, 256), (256, 512), (512, 1024), (1024, 1536), (1536, 2048)]
+DA1, DA3 = 0, 1
+
+A1_LOADS = [(0, 256), (256, 512), (512, 768), (768, 1024), (1024, 1536), (1536, 2048)]
+A3_LOADS = [(0, 256), (256, 512), (512, 1024), (1024, 1536), (1536, 2048)]
+
+TANH_LEAD = 3
+SILU_LEAD = 2
+TERM_LEAD = 1
 LAG = 2
+
 SUM_BANKS = 5
 TURN_BANKS = 2
-TH_LEAD = 3
-GATED_LEAD = 3
-TERM_LEAD = 1
-NEG_LEAD = 2
-QUANTIZE_AT = (6, 10, 14)
-PIECE = 256
+
+REST_ON_GPSIMD = range(5, 12, 2)
+
+FIRST_PIECE = 512
 STORES = [(0, 384), (384, 704), (704, 896), (896, 1024)]
 
 
@@ -55,15 +61,15 @@ def tile_moe_bdx_glu_silu_kernel(
         w13_w = keep.tile([P, 2 * E * 2 * K], U8, name="w13_w", align_bytes=64)
         w13_s = keep.tile([P, 2 * E * K], U8, name="w13_s", align_bytes=64)
         gate_rows = keep.tile([P, P], F32, name="gate_rows")
-        gate_cols = keep.tile([P, TILES], F32, name="gate_cols")
+        half_gate = keep.tile([P, TILES], F32, name="half_gate")
         ident = keep.tile([P, P], F32, name="ident")
         dx = keep.tile([P, E * C], F32, name="dx")
-        a1_sb = [keep.tile([P, 4, hi - lo], F32, name="a1_sb%d" % lo) for lo, hi in A1_CHUNKS]
-        a3_sb = [keep.tile([P, 4, hi - lo], F32, name="a3_sb%d" % lo) for lo, hi in A3_CHUNKS]
-        g_w = [keep.tile([P, C], U32, name="g_w%d" % i, align_bytes=64) for i in range(E)]
-        g_s = [keep.tile([P, C], U8, name="g_s%d" % i, align_bytes=64) for i in range(E)]
-        sums = [psum.tile([P, H], F32, name="sums%d" % i) for i in range(SUM_BANKS)]
-        turns = [psum.tile([P, H], F32, name="turns%d" % i) for i in range(TURN_BANKS)]
+        a1_sb = [keep.tile([P, PACK, hi - lo], F32, name="a1_sb%d" % lo) for lo, hi in A1_LOADS]
+        a3_sb = [keep.tile([P, PACK, hi - lo], F32, name="a3_sb%d" % lo) for lo, hi in A3_LOADS]
+        g_w = [keep.tile([P, C], U32, name="g_w%d" % e, align_bytes=64) for e in range(E)]
+        g_s = [keep.tile([P, C], U8, name="g_s%d" % e, align_bytes=64) for e in range(E)]
+        sums = [psum.tile([P, H], F32, name="sums%d" % b) for b in range(SUM_BANKS)]
+        turns = [psum.tile([P, H], F32, name="turns%d" % b) for b in range(TURN_BANKS)]
 
         nc.gpsimd.memset(dy_s[:].bitcast(I32), 0)
         for plane in (w2_s, w13_s):
@@ -71,102 +77,99 @@ def tile_moe_bdx_glu_silu_kernel(
         nc.gpsimd.memset(gate_rows[:], 0.0)
         make_identity(nc, ident[:])
 
-        def load_scales(plane_view, scales):
-            rows = scales.rearrange("e s f c -> f (e s) c")
+        def load_scales(plane_view, rows):
             for q in range(4):
                 nc.sync.dma_start(out=plane_view[32 * q : 32 * q + 4].bitcast(I32), in_=rows[4 * q : 4 * q + 4].bitcast(I32))
 
-        def load_saved(dst, src, chunks, c):
-            lo, hi = chunks[c]
-            nc.sync.dma_start(out=dst[c][:], in_=src[:, lo:hi].rearrange("(p d) s -> p d s", d=4))
+        def load_a1(c):
+            lo, hi = A1_LOADS[c]
+            nc.sync.dma_start(out=a1_sb[c][:], in_=a1[:, lo:hi].rearrange("(p d) s -> p d s", d=PACK))
 
-        def saved(tiles, chunks, t):
-            c = max(i for i, (lo, hi) in enumerate(chunks) if lo <= t * P)
-            lo = t * P - chunks[c][0]
-            return tiles[c][:, :, lo : lo + P]
+        def load_a3(c):
+            lo, hi = A3_LOADS[c]
+            nc.sync.dma_start(out=a3_sb[c][:], in_=a3[:, lo:hi].rearrange("(p d) s -> p d s", d=PACK))
 
-        def load_w2(e0, e1):
+        def load_w2(first_expert, end_expert):
             nc.sync.dma_start(
-                out=w2_w[:].rearrange("p (e c) -> p e c", e=E)[:, e0:e1].bitcast(I32),
-                in_=w2_words.rearrange("e s p c -> p (e s) c")[:, e0:e1].bitcast(I32),
+                out=w2_w[:].rearrange("p (e c) -> p e c", e=E)[:, first_expert:end_expert].bitcast(I32),
+                in_=w2_words.rearrange("e s p c -> p (e s) c")[:, first_expert:end_expert].bitcast(I32),
             )
+
+        def saved(tiles, loads, t):
+            c = max(n for n, (lo, hi) in enumerate(loads) if lo <= t * P)
+            lo = t * P - loads[c][0]
+            return tiles[c][:, :, lo : lo + P]
 
         w13_w_view = w13_w[:].rearrange("p (a e c) -> p a e c", a=2, e=E)
         w13_s_view = w13_s[:].rearrange("p (a e c) -> p a e c", a=2, e=E)
         nc.sync.dma_start(offs_sb[:], offs)
-        for q in range(4):
-            nc.sync.dma_start(out=dy_s[32 * q : 32 * q + 4, :].bitcast(I32), in_=dy_scales[0, 4 * q : 4 * q + 4, :].bitcast(I32))
-        load_saved(a1_sb, a1, A1_CHUNKS, 0)
+        load_scales(dy_s[:], dy_scales[0])
+        load_a1(0)
+        nc.sync.dma_start(out=gate_rows[0:TILES, :], in_=gate[0].rearrange("(t s) -> t s", s=P))
         nc.sync.dma_start(out=dy_w[:], in_=dy_words[0].rearrange("p t d -> p (t d)").bitcast(I32))
-        nc.sync.dma_start(out=gate_rows[0:TILES, :], in_=gate[0].rearrange("(c p) -> c p", p=P))
-        load_saved(a3_sb, a3, A3_CHUNKS, 0)
-        load_saved(a1_sb, a1, A1_CHUNKS, 1)
-        load_scales(w2_s[:].rearrange("p (e c) -> p e c", e=E), w2_scales)
-        load_w2(0, 4)
-        load_saved(a3_sb, a3, A3_CHUNKS, 1)
-        load_saved(a1_sb, a1, A1_CHUNKS, 2)
-        load_saved(a3_sb, a3, A3_CHUNKS, 2)
-        load_saved(a1_sb, a1, A1_CHUNKS, 3)
-        load_saved(a3_sb, a3, A3_CHUNKS, 3)
-        load_saved(a1_sb, a1, A1_CHUNKS, 4)
-        load_saved(a3_sb, a3, A3_CHUNKS, 4)
-        load_scales(w13_s_view[:, 0], w1_scales)
-        load_scales(w13_s_view[:, 1], w3_scales)
-        for a, words in enumerate((w1_words, w3_words)):
-            nc.sync.dma_start(out=w13_w_view[:, a].bitcast(I32), in_=words.rearrange("e s p c -> p (e s) c").bitcast(I32))
+        load_a3(0)
+        load_a1(1)
+        load_scales(w2_s[:].rearrange("p (e c) -> p e c", e=E), w2_scales.rearrange("e s f c -> f (e s) c"))
+        load_w2(0, E // 2)
+        load_a1(2)
+        load_a3(1)
+        load_a1(3)
+        load_a3(2)
+        load_w2(E // 2, E)
+        load_a1(4)
+        load_a3(3)
+        load_a1(5)
+        load_a3(4)
+        for a, weight_scales in ((DA1, w1_scales), (DA3, w3_scales)):
+            load_scales(w13_s_view[:, a], weight_scales.rearrange("e s f c -> f (e s) c"))
+        for a, weight_words in ((DA1, w1_words), (DA3, w3_words)):
+            nc.sync.dma_start(out=w13_w_view[:, a].bitcast(I32), in_=weight_words.rearrange("e s p c -> p (e s) c").bitcast(I32))
         nc.sync.dma_start(pos1_sb[:], pos1)
         nc.sync.dma_start(pos2_sb[:], pos2)
 
         for e in range(E):
-            nc.vector.tensor_copy(g_s[e][:], dy_s[:].indirect(offs_sb[:, e * C // 16 : (e + 1) * C // 16]))
-            nc.vector.tensor_copy(g_w[e][:], dy_w[:].bitcast(U32).indirect(offs_sb[:, e * C // 16 : (e + 1) * C // 16]))
+            entries = offs_sb[:, e * C // 16 : (e + 1) * C // 16]
+            nc.vector.tensor_copy(g_s[e][:], dy_s[:].indirect(entries))
+            nc.vector.tensor_copy(g_w[e][:], dy_w[:].bitcast(U32).indirect(entries))
 
         spare = psum.tile([P, C], F32, name="spare")
         nc.tensor.transpose(spare[:, 0:P], gate_rows[:], ident[:])
-        nc.scalar.activation(out=gate_cols[:], in_=spare[:, 0:TILES], func=ACT.Copy, scale=0.5)
+        nc.scalar.activation(out=half_gate[:], in_=spare[:, 0:TILES], func=ACT.Copy, scale=0.5)
 
-        th, gated, rest, term = {}, {}, {}, {}
+        tanh, gated, silu, rest, term = {}, {}, {}, {}, {}
 
-        def make_th(t):
+        def make_tanh(t):
             bank = turns[t % TURN_BANKS]
-            v = saved(a1_sb, A1_CHUNKS, t)
-            for d in range(4):
+            v = saved(a1_sb, A1_LOADS, t)
+            for d in range(PACK):
                 nc.tensor.transpose(bank[:, d * P : (d + 1) * P], v[:, d, :], ident[:])
-            th[t] = work.tile([P, H], F32, name="th", bufs=4)
-            nc.scalar.activation(out=th[t][:], in_=bank[:], func=ACT.Tanh, scale=0.5)
+            tanh[t] = work.tile([P, H], F32, name="tanh", bufs=4)
+            nc.scalar.activation(out=tanh[t][:], in_=bank[:], func=ACT.Tanh, scale=0.5)
 
         def make_gated(t):
             gated[t] = work.tile([P, H], F32, name="gated", bufs=6)
-            hg = gate_cols[:, t : t + 1]
-            nc.scalar.activation(out=gated[t][:], in_=th[t][:], func=ACT.Identity, scale=hg, bias=hg)
+            factor = half_gate[:, t : t + 1]
+            nc.scalar.activation(out=gated[t][:], in_=tanh[t][:], func=ACT.Identity, scale=factor, bias=factor)
 
-        def on_gpsimd(t):
-            return t in (5, 7, 9, 11, 13)
-
-        def make_neg(t):
-            neg = work.tile([P, 4, P], F32, name="neg", bufs=4)
-            nc.scalar.activation(out=neg[:], in_=saved(a1_sb, A1_CHUNKS, t), func=ACT.Silu, scale=-1.0)
-            if on_gpsimd(t):
-                rest[t] = neg
-            else:
-                rest[t] = work.tile([P, 4, P], F32, name="rest", bufs=4)
-                nc.scalar.activation(out=rest[t][:], in_=neg[:], func=ACT.Copy, scale=-1.0, bias=1.0)
+        def make_silu(t):
+            silu[t] = work.tile([P, PACK, P], F32, name="silu", bufs=4)
+            nc.scalar.activation(out=silu[t][:], in_=saved(a1_sb, A1_LOADS, t), func=ACT.Silu, scale=-1.0)
+            if t not in REST_ON_GPSIMD:
+                rest[t] = work.tile([P, PACK, P], F32, name="rest", bufs=4)
+                nc.scalar.activation(out=rest[t][:], in_=silu[t][:], func=ACT.Copy, scale=-1.0, bias=1.0)
 
         def make_term(t):
-            term[t] = work.tile([P, 4, P], F32, name="term", bufs=6)
-            if on_gpsimd(t):
-                nc.gpsimd.tensor_scalar(out=term[t][:], in0=rest[t][:], scalar1=-1.0, scalar2=1.0, op0=ALU.mult, op1=ALU.add)
+            term[t] = work.tile([P, PACK, P], F32, name="term", bufs=6)
+            if t in REST_ON_GPSIMD:
                 rest[t] = term[t]
-            nc.gpsimd.tensor_tensor(out=term[t][:], in0=rest[t][:], in1=saved(a3_sb, A3_CHUNKS, t), op=ALU.mult)
-
-        def sum_bank(t):
-            return sums[t % SUM_BANKS]
+                nc.gpsimd.tensor_scalar(out=rest[t][:], in0=silu[t][:], scalar1=-1.0, scalar2=1.0, op0=ALU.mult, op1=ALU.add)
+            nc.gpsimd.tensor_tensor(out=term[t][:], in0=rest[t][:], in1=saved(a3_sb, A3_LOADS, t), op=ALU.mult)
 
         def first_product(t):
             e, j = divmod(t, PER_EXPERT)
             slots = slice(j * P, (j + 1) * P)
             nc.tensor.matmul_mx(
-                out=sum_bank(t)[:],
+                out=sums[t % SUM_BANKS][:],
                 lhsT=g_w[e][:, slots].bitcast(E5M2X4),
                 lhsT_scale=g_s[e][:, slots],
                 rhs=w2_w[:, e * 2 * H : (e + 1) * 2 * H].bitcast(E2M1X4),
@@ -175,89 +178,93 @@ def tile_moe_bdx_glu_silu_kernel(
                 stop=True,
             )
 
-        def common(t):
-            bank = sum_bank(t)
-            pr = work.tile([P, 4, P], F32, name="pr", bufs=3)
+        def make_common(t):
+            bank = sums[t % SUM_BANKS]
+            common = work.tile([P, PACK, P], F32, name="common", bufs=3)
             nc.vector.tensor_tensor(
-                out=pr[:], in0=bank[:].rearrange("s (p d) -> s d p", d=4), in1=gated[t][:].rearrange("s (d p) -> s d p", d=4), op=ALU.mult
+                out=common[:],
+                in0=bank[:].rearrange("s (p d) -> s d p", d=PACK),
+                in1=gated[t][:].rearrange("s (d p) -> s d p", d=PACK),
+                op=ALU.mult,
             )
-            for d in range(4):
-                nc.tensor.transpose(bank[:, d * P : (d + 1) * P], pr[:, d, :], ident[:])
+            for d in range(PACK):
+                nc.tensor.transpose(bank[:, d * P : (d + 1) * P], common[:, d, :], ident[:])
 
         grouped, codes, scales = {}, {}, {}
 
         def last_product(t, a):
             e, j = divmod(t, PER_EXPERT)
             if e not in grouped:
-                grouped[e] = work.tile([P, 2 * C * 4], BF16, name="grouped", bufs=E, align_bytes=64)
+                grouped[e] = work.tile([P, 2 * C * PACK], BF16, name="grouped", bufs=E, align_bytes=64)
                 codes[e] = work.tile([P, 2 * C], U32, name="codes", bufs=E, align_bytes=64)
                 scales[e] = work.tile([P, 2 * C], U8, name="scales", bufs=E, align_bytes=64)
-            turned = sum_bank(t)[:].rearrange("p (d c i) -> p c d i", d=4, i=2)
-            factor = saved(a1_sb, A1_CHUNKS, t) if a == 1 else term[t][:]
-            lo = 4 * (a * C + j * P)
+            factor = saved(a1_sb, A1_LOADS, t) if a == DA3 else term[t][:]
+            lo = PACK * (a * C + j * P)
             nc.vector.tensor_tensor(
-                out=grouped[e][:, lo : lo + 4 * P].rearrange("p (c i d) -> p c d i", d=4, i=2),
-                in0=turned,
-                in1=factor.rearrange("p d (c i) -> p c d i", i=2),
+                out=grouped[e][:, lo : lo + PACK * P].rearrange("p (pair two d) -> p pair d two", d=PACK, two=2),
+                in0=sums[t % SUM_BANKS][:].rearrange("p (d pair two) -> p pair d two", d=PACK, two=2),
+                in1=factor.rearrange("p d (pair two) -> p pair d two", two=2),
                 op=ALU.mult,
             )
 
-        def quantize(e, c0, c1):
-            nc.vector.quantize_mx(out=codes[e][:, c0:c1].bitcast(E5M2X4), scales=scales[e][:, c0:c1], in_=grouped[e][:, 4 * c0 : 4 * c1])
+        def quantize(e, lo, hi):
+            nc.vector.quantize_mx(
+                out=codes[e][:, lo:hi].bitcast(E5M2X4), scales=scales[e][:, lo:hi], in_=grouped[e][:, PACK * lo : PACK * hi]
+            )
 
-        def finish(e):
+        def second_product(e):
             acc = (spare, turns[0], turns[1], spare)[e]
-            for a in (1, 0):
+            for a in (DA3, DA1):
                 nc.tensor.matmul_mx(
                     out=acc[:],
                     lhsT=w13_w_view[:, a, e, :].bitcast(E2M1X4),
                     lhsT_scale=w13_s_view[:, a, e, :],
                     rhs=codes[e][:, a * C : (a + 1) * C].bitcast(E5M2X4),
                     rhs_scale=scales[e][:, a * C : (a + 1) * C],
-                    start=(a == 1),
-                    stop=(a == 0),
+                    start=(a == DA3),
+                    stop=(a == DA1),
                 )
             if e < E - 1:
                 nc.scalar.copy(out=dx[:, e * C : (e + 1) * C], in_=acc[:])
             else:
                 nc.vector.tensor_copy(out=dx[:, e * C : (e + 1) * C], in_=acc[:])
 
-        for step in range(-4, TILES + LAG):
-            if 0 <= step + TH_LEAD < TILES:
-                make_th(step + TH_LEAD)
-            if 0 <= step + GATED_LEAD < TILES:
-                make_gated(step + GATED_LEAD)
-            if 0 <= step + NEG_LEAD < TILES:
-                make_neg(step + NEG_LEAD)
+        for step in range(-TANH_LEAD, TILES):
+            if step + TANH_LEAD < TILES:
+                make_tanh(step + TANH_LEAD)
+                make_gated(step + TANH_LEAD)
+            if 0 <= step + SILU_LEAD < TILES:
+                make_silu(step + SILU_LEAD)
             if 0 <= step + TERM_LEAD < TILES:
                 make_term(step + TERM_LEAD)
             if 0 <= step + 1 < TILES:
                 first_product(step + 1)
-            if 0 <= step < TILES:
-                common(step)
-            if 0 <= step - LAG < TILES - 2:
-                last_product(step - LAG, 1)
-                last_product(step - LAG, 0)
-            if step in QUANTIZE_AT:
-                quantize(QUANTIZE_AT.index(step), 0, 2 * C)
+            if 0 <= step:
+                make_common(step)
+            if 0 <= step - LAG:
+                last_product(step - LAG, DA3)
+                last_product(step - LAG, DA1)
+            whole_experts, place = divmod(step - LAG, PER_EXPERT)
+            if whole_experts >= 1 and place == 0:
+                quantize(whole_experts - 1, 0, 2 * C)
+
         last = E - 1
-        last_product(TILES - 2, 1)
-        last_product(TILES - 2, 0)
-        for a in (1, 0):
-            quantize(last, a * C, a * C + 2 * P)
-        last_product(TILES - 1, 1)
-        last_product(TILES - 1, 0)
-        quantize(last, C + 2 * P, 2 * C)
-        quantize(last, 2 * P, 3 * P)
-        quantize(last, 3 * P, C)
+        last_product(TILES - 2, DA3)
+        last_product(TILES - 2, DA1)
+        last_product(TILES - 1, DA3)
+        quantize(last, DA1 * C, DA1 * C + 2 * P)
+        quantize(last, DA3 * C, DA3 * C + C)
+        last_product(TILES - 1, DA1)
+        quantize(last, DA1 * C + 2 * P, DA1 * C + 3 * P)
+        quantize(last, DA1 * C + 3 * P, DA1 * C + C)
         for e in range(E):
-            finish(e)
+            second_product(e)
 
         first = keep.tile([P, T], F32, name="first")
         total = keep.tile([P, T], F32, name="total")
-        for c in range(0, T, 2 * PIECE):
-            nc.vector.tensor_copy(first[:, c : c + 2 * PIECE], dx[:].indirect(pos1_sb[:, c // 16 : (c + 2 * PIECE) // 16]))
+        for lo in range(0, T, FIRST_PIECE):
+            hi = lo + FIRST_PIECE
+            nc.vector.tensor_copy(first[:, lo:hi], dx[:].indirect(pos1_sb[:, lo // 16 : hi // 16]))
         for lo, hi in STORES:
-            cols = slice(lo, hi)
-            nc.vector.tensor_tensor(total[:, cols], dx[:].indirect(pos2_sb[:, lo // 16 : hi // 16]), first[:, cols], ALU.add)
-            nc.sync.dma_start(out=out[:, cols], in_=total[:, cols])
+            nc.vector.tensor_tensor(total[:, lo:hi], dx[:].indirect(pos2_sb[:, lo // 16 : hi // 16]), first[:, lo:hi], ALU.add)
+            nc.sync.dma_start(out=out[:, lo:hi], in_=total[:, lo:hi])

@@ -35,7 +35,7 @@ LAG = 2
 SUM_BANKS = 5
 TURN_BANKS = 2
 
-REST_ON_GPSIMD = range(5, 12, 2)
+REST_ON_GPSIMD = (6, 7, 10, 11)
 
 FIRST_PIECE = 512
 STORES = [(0, 384), (384, 704), (704, 896), (896, 1024)]
@@ -155,11 +155,11 @@ def tile_moe_bdx_glu_silu_kernel(
             silu[t] = work.tile([P, PACK, P], F32, name="silu", bufs=4)
             nc.scalar.activation(out=silu[t][:], in_=saved(a1_sb, A1_LOADS, t), func=ACT.Silu, scale=-1.0)
             if t not in REST_ON_GPSIMD:
-                rest[t] = work.tile([P, PACK, P], F32, name="rest", bufs=4)
+                rest[t] = work.tile([P, PACK, P], F32, name="rest", bufs=5)
                 nc.scalar.activation(out=rest[t][:], in_=silu[t][:], func=ACT.Copy, scale=-1.0, bias=1.0)
 
         def make_term(t):
-            term[t] = work.tile([P, PACK, P], F32, name="term", bufs=6)
+            term[t] = work.tile([P, PACK, P], F32, name="term", bufs=2)
             if t in REST_ON_GPSIMD:
                 rest[t] = term[t]
                 nc.gpsimd.tensor_scalar(out=rest[t][:], in0=silu[t][:], scalar1=-1.0, scalar2=1.0, op0=ALU.mult, op1=ALU.add)

@@ -35,7 +35,9 @@ LAG = 2
 SUM_BANKS = 5
 TURN_BANKS = 2
 
-REST_ON_GPSIMD = (6, 7, 10, 11)
+REST_ON_GPSIMD = range(2, 11, 4)
+
+GATHERS = [(0, 768), (768, 1408), (1408, 2048)]
 
 FIRST_PIECE = 512
 STORES = [(0, 384), (384, 704), (704, 896), (896, 1024)]
@@ -66,8 +68,8 @@ def tile_moe_bdx_glu_silu_kernel(
         dx = keep.tile([P, E * C], F32, name="dx")
         a1_sb = [keep.tile([P, PACK, hi - lo], F32, name="a1_sb%d" % lo) for lo, hi in A1_LOADS]
         a3_sb = [keep.tile([P, PACK, hi - lo], F32, name="a3_sb%d" % lo) for lo, hi in A3_LOADS]
-        g_w = [keep.tile([P, C], U32, name="g_w%d" % e, align_bytes=64) for e in range(E)]
-        g_s = [keep.tile([P, C], U8, name="g_s%d" % e, align_bytes=64) for e in range(E)]
+        g_w = keep.tile([P, E * C], U32, name="g_w", align_bytes=64)
+        g_s = keep.tile([P, E * C], U8, name="g_s", align_bytes=64)
         sums = [psum.tile([P, H], F32, name="sums%d" % b) for b in range(SUM_BANKS)]
         turns = [psum.tile([P, H], F32, name="turns%d" % b) for b in range(TURN_BANKS)]
 
@@ -127,10 +129,10 @@ def tile_moe_bdx_glu_silu_kernel(
         nc.sync.dma_start(pos1_sb[:], pos1)
         nc.sync.dma_start(pos2_sb[:], pos2)
 
-        for e in range(E):
-            entries = offs_sb[:, e * C // 16 : (e + 1) * C // 16]
-            nc.vector.tensor_copy(g_s[e][:], dy_s[:].indirect(entries))
-            nc.vector.tensor_copy(g_w[e][:], dy_w[:].bitcast(U32).indirect(entries))
+        for lo, hi in GATHERS:
+            nc.vector.tensor_copy(g_s[:, lo:hi], dy_s[:].indirect(offs_sb[:, lo // 16 : hi // 16]))
+        for lo, hi in GATHERS:
+            nc.vector.tensor_copy(g_w[:, lo:hi], dy_w[:].bitcast(U32).indirect(offs_sb[:, lo // 16 : hi // 16]))
 
         spare = psum.tile([P, C], F32, name="spare")
         nc.tensor.transpose(spare[:, 0:P], gate_rows[:], ident[:])
@@ -159,19 +161,24 @@ def tile_moe_bdx_glu_silu_kernel(
                 nc.scalar.activation(out=rest[t][:], in_=silu[t][:], func=ACT.Copy, scale=-1.0, bias=1.0)
 
         def make_term(t):
-            term[t] = work.tile([P, PACK, P], F32, name="term", bufs=2)
+            if t == 0:
+                term[t] = keep.tile([P, PACK, P], F32, name="dy_w", align_bytes=64)
+            elif t == TILES - 1:
+                term[t] = keep.tile([P, PACK, P], F32, name="last_term")
+            else:
+                term[t] = work.tile([P, PACK, P], F32, name="term", bufs=2)
             if t in REST_ON_GPSIMD:
                 rest[t] = term[t]
                 nc.gpsimd.tensor_scalar(out=rest[t][:], in0=silu[t][:], scalar1=-1.0, scalar2=1.0, op0=ALU.mult, op1=ALU.add)
             nc.gpsimd.tensor_tensor(out=term[t][:], in0=rest[t][:], in1=saved(a3_sb, A3_LOADS, t), op=ALU.mult)
 
         def first_product(t):
-            e, j = divmod(t, PER_EXPERT)
-            slots = slice(j * P, (j + 1) * P)
+            e = t // PER_EXPERT
+            slots = slice(t * P, (t + 1) * P)
             nc.tensor.matmul_mx(
                 out=sums[t % SUM_BANKS][:],
-                lhsT=g_w[e][:, slots].bitcast(E5M2X4),
-                lhsT_scale=g_s[e][:, slots],
+                lhsT=g_w[:, slots].bitcast(E5M2X4),
+                lhsT_scale=g_s[:, slots],
                 rhs=w2_w[:, e * 2 * H : (e + 1) * 2 * H].bitcast(E2M1X4),
                 rhs_scale=w2_s[:, e * H : (e + 1) * H],
                 start=True,
@@ -192,18 +199,26 @@ def tile_moe_bdx_glu_silu_kernel(
 
         grouped, codes, scales = {}, {}, {}
 
-        def last_product(t, a):
+        def column(e, a, j):
+            if e < E - 1:
+                return a * C + j * P
+            if a == DA3:
+                return C - P + j * P
+            return j * P if j < PER_EXPERT - 1 else 2 * C - P
+
+        def last_product(t, a, first_slot=0, end_slot=P):
             e, j = divmod(t, PER_EXPERT)
             if e not in grouped:
                 grouped[e] = work.tile([P, 2 * C * PACK], BF16, name="grouped", bufs=E, align_bytes=64)
                 codes[e] = work.tile([P, 2 * C], U32, name="codes", bufs=E, align_bytes=64)
                 scales[e] = work.tile([P, 2 * C], U8, name="scales", bufs=E, align_bytes=64)
             factor = saved(a1_sb, A1_LOADS, t) if a == DA3 else term[t][:]
-            lo = PACK * (a * C + j * P)
+            lo = PACK * column(e, a, j)
+            pairs = slice(first_slot // 2, end_slot // 2)
             nc.vector.tensor_tensor(
-                out=grouped[e][:, lo : lo + PACK * P].rearrange("p (pair two d) -> p pair d two", d=PACK, two=2),
-                in0=sums[t % SUM_BANKS][:].rearrange("p (d pair two) -> p pair d two", d=PACK, two=2),
-                in1=factor.rearrange("p d (pair two) -> p pair d two", two=2),
+                out=grouped[e][:, lo : lo + PACK * P].rearrange("p (pair two d) -> p pair d two", d=PACK, two=2)[:, pairs],
+                in0=sums[t % SUM_BANKS][:].rearrange("p (d pair two) -> p pair d two", d=PACK, two=2)[:, pairs],
+                in1=factor.rearrange("p d (pair two) -> p pair d two", two=2)[:, pairs],
                 op=ALU.mult,
             )
 
@@ -212,22 +227,22 @@ def tile_moe_bdx_glu_silu_kernel(
                 out=codes[e][:, lo:hi].bitcast(E5M2X4), scales=scales[e][:, lo:hi], in_=grouped[e][:, PACK * lo : PACK * hi]
             )
 
+        def second_pass(acc, e, a, lo, first_pass):
+            nc.tensor.matmul_mx(
+                out=acc[:],
+                lhsT=w13_w_view[:, a, e, :].bitcast(E2M1X4),
+                lhsT_scale=w13_s_view[:, a, e, :],
+                rhs=codes[e][:, lo : lo + C].bitcast(E5M2X4),
+                rhs_scale=scales[e][:, lo : lo + C],
+                start=first_pass,
+                stop=not first_pass,
+            )
+
         def second_product(e):
-            acc = (spare, turns[0], turns[1], spare)[e]
-            for a in (DA3, DA1):
-                nc.tensor.matmul_mx(
-                    out=acc[:],
-                    lhsT=w13_w_view[:, a, e, :].bitcast(E2M1X4),
-                    lhsT_scale=w13_s_view[:, a, e, :],
-                    rhs=codes[e][:, a * C : (a + 1) * C].bitcast(E5M2X4),
-                    rhs_scale=scales[e][:, a * C : (a + 1) * C],
-                    start=(a == DA3),
-                    stop=(a == DA1),
-                )
-            if e < E - 1:
-                nc.scalar.copy(out=dx[:, e * C : (e + 1) * C], in_=acc[:])
-            else:
-                nc.vector.tensor_copy(out=dx[:, e * C : (e + 1) * C], in_=acc[:])
+            acc = spare if e == 0 else sums[(TILES - E + e) % SUM_BANKS]
+            second_pass(acc, e, DA3, DA3 * C, True)
+            second_pass(acc, e, DA1, DA1 * C, False)
+            nc.scalar.copy(out=dx[:, e * C : (e + 1) * C], in_=acc[:])
 
         for step in range(-TANH_LEAD, TILES):
             if step + TANH_LEAD < TILES:
@@ -252,13 +267,22 @@ def tile_moe_bdx_glu_silu_kernel(
         last_product(TILES - 2, DA3)
         last_product(TILES - 2, DA1)
         last_product(TILES - 1, DA3)
-        quantize(last, DA1 * C, DA1 * C + 2 * P)
-        quantize(last, DA3 * C, DA3 * C + C)
-        last_product(TILES - 1, DA1)
-        quantize(last, DA1 * C + 2 * P, DA1 * C + 3 * P)
-        quantize(last, DA1 * C + 3 * P, DA1 * C + C)
-        for e in range(E):
+        quantize(last, 0, 2 * P)
+        quantize(last, C - P, 2 * C - P)
+        quantize(last, 2 * P, 3 * P)
+        last_product(TILES - 1, DA1, 0, P // 2)
+        last_product(TILES - 1, DA1, P // 2, P)
+        quantize(last, 2 * C - P, 2 * C - P // 2)
+        quantize(last, 2 * C - P // 2, 2 * C)
+        for e in range(last):
             second_product(e)
+        early, final = turns
+        second_pass(final, last, DA3, C - P, True)
+        second_pass(early, last, DA3, C - P, True)
+        second_pass(early, last, DA1, 0, False)
+        nc.scalar.copy(out=dx[:, last * C : E * C - P], in_=early[:, 0 : C - P])
+        second_pass(final, last, DA1, C, False)
+        nc.vector.tensor_copy(out=dx[:, E * C - P : E * C], in_=final[:, C - P : C])
 
         first = keep.tile([P, T], F32, name="first")
         total = keep.tile([P, T], F32, name="total")

@@ -24,7 +24,7 @@ TILES = E * C // P
 PER_EXPERT = C // P
 DA1, DA3 = 0, 1
 
-A1_LOADS = [(0, 256), (256, 512), (512, 768), (768, 1024), (1024, 1536), (1536, 2048)]
+A1_LOADS = [(0, 128), (128, 384), (384, 768), (768, 1024), (1024, 1536), (1536, 2048)]
 A3_LOADS = [(0, 256), (256, 512), (512, 1024), (1024, 1536), (1536, 2048)]
 
 TANH_LEAD = 3
@@ -35,7 +35,8 @@ LAG = 2
 SUM_BANKS = 5
 TURN_BANKS = 2
 
-REST_ON_GPSIMD = range(2, 11, 4)
+TERM_BUFFERS = 2
+REST_ON_GPSIMD = (PER_EXPERT + LAG, 2 * PER_EXPERT + LAG)
 
 GATHERS = [(0, 768), (768, 1408), (1408, 2048)]
 
@@ -108,14 +109,14 @@ def tile_moe_bdx_glu_silu_kernel(
         load_scales(dy_s[:], dy_scales[0])
         load_a1(0)
         nc.sync.dma_start(out=gate_rows[0:TILES, :], in_=gate[0].rearrange("(t s) -> t s", s=P))
-        nc.sync.dma_start(out=dy_w[:], in_=dy_words[0].rearrange("p t d -> p (t d)").bitcast(I32))
-        load_a3(0)
         load_a1(1)
+        nc.sync.dma_start(out=dy_w[:], in_=dy_words[0].rearrange("p t d -> p (t d)").bitcast(I32))
+        load_a1(2)
         load_scales(w2_s[:].rearrange("p (e c) -> p e c", e=E), w2_scales.rearrange("e s f c -> f (e s) c"))
         load_w2(0, E // 2)
-        load_a1(2)
-        load_a3(1)
+        load_a3(0)
         load_a1(3)
+        load_a3(1)
         load_a3(2)
         load_w2(E // 2, E)
         load_a1(4)
@@ -162,11 +163,11 @@ def tile_moe_bdx_glu_silu_kernel(
 
         def make_term(t):
             if t == 0:
-                term[t] = keep.tile([P, PACK, P], F32, name="dy_w", align_bytes=64)
+                term[t] = keep.tile([P, PACK, P], F32, name="first_term", tag="dy_w", align_bytes=64)
             elif t == TILES - 1:
                 term[t] = keep.tile([P, PACK, P], F32, name="last_term")
             else:
-                term[t] = work.tile([P, PACK, P], F32, name="term", bufs=2)
+                term[t] = work.tile([P, PACK, P], F32, name="term", bufs=TERM_BUFFERS)
             if t in REST_ON_GPSIMD:
                 rest[t] = term[t]
                 nc.gpsimd.tensor_scalar(out=rest[t][:], in0=silu[t][:], scalar1=-1.0, scalar2=1.0, op0=ALU.mult, op1=ALU.add)
@@ -198,13 +199,15 @@ def tile_moe_bdx_glu_silu_kernel(
                 nc.tensor.transpose(bank[:, d * P : (d + 1) * P], common[:, d, :], ident[:])
 
         grouped, codes, scales = {}, {}, {}
+        last = E - 1
+        most = C - P
 
         def column(e, a, j):
-            if e < E - 1:
+            if e < last:
                 return a * C + j * P
             if a == DA3:
-                return C - P + j * P
-            return j * P if j < PER_EXPERT - 1 else 2 * C - P
+                return most + j * P
+            return j * P if j < PER_EXPERT - 1 else most + C
 
         def last_product(t, a, first_slot=0, end_slot=P):
             e, j = divmod(t, PER_EXPERT)
@@ -238,8 +241,7 @@ def tile_moe_bdx_glu_silu_kernel(
                 stop=not first_pass,
             )
 
-        def second_product(e):
-            acc = spare if e == 0 else sums[(TILES - E + e) % SUM_BANKS]
+        def second_product(e, acc):
             second_pass(acc, e, DA3, DA3 * C, True)
             second_pass(acc, e, DA1, DA1 * C, False)
             nc.scalar.copy(out=dx[:, e * C : (e + 1) * C], in_=acc[:])
@@ -263,26 +265,29 @@ def tile_moe_bdx_glu_silu_kernel(
             if whole_experts >= 1 and place == 0:
                 quantize(whole_experts - 1, 0, 2 * C)
 
-        last = E - 1
+        final_da1 = column(last, DA1, PER_EXPERT - 1)
         last_product(TILES - 2, DA3)
         last_product(TILES - 2, DA1)
         last_product(TILES - 1, DA3)
         quantize(last, 0, 2 * P)
-        quantize(last, C - P, 2 * C - P)
-        quantize(last, 2 * P, 3 * P)
+        quantize(last, most, most + C)
+        quantize(last, 2 * P, most)
         last_product(TILES - 1, DA1, 0, P // 2)
         last_product(TILES - 1, DA1, P // 2, P)
-        quantize(last, 2 * C - P, 2 * C - P // 2)
-        quantize(last, 2 * C - P // 2, 2 * C)
-        for e in range(last):
-            second_product(e)
+        quantize(last, final_da1, final_da1 + P // 2)
+        quantize(last, final_da1 + P // 2, final_da1 + P)
+
+        second_product(0, sums[(TILES - 3) % SUM_BANKS])
+        second_product(1, sums[(TILES - 2) % SUM_BANKS])
+        second_product(2, spare)
+
         early, final = turns
-        second_pass(final, last, DA3, C - P, True)
-        second_pass(early, last, DA3, C - P, True)
+        second_pass(final, last, DA3, most, True)
+        second_pass(early, last, DA3, most, True)
         second_pass(early, last, DA1, 0, False)
-        nc.scalar.copy(out=dx[:, last * C : E * C - P], in_=early[:, 0 : C - P])
-        second_pass(final, last, DA1, C, False)
-        nc.vector.tensor_copy(out=dx[:, E * C - P : E * C], in_=final[:, C - P : C])
+        nc.scalar.copy(out=dx[:, last * C : last * C + most], in_=early[:, 0:most])
+        second_pass(final, last, DA1, final_da1 - most, False)
+        nc.vector.tensor_copy(out=dx[:, last * C + most : E * C], in_=final[:, most:C])
 
         first = keep.tile([P, T], F32, name="first")
         total = keep.tile([P, T], F32, name="total")

@@ -35,7 +35,7 @@ LAG = 2
 SUM_BANKS = 5
 TURN_BANKS = 2
 
-TERM_BUFFERS = 2
+TERM_BUFFERS = (1, 2)
 REST_ON_GPSIMD = (PER_EXPERT + LAG, 2 * PER_EXPERT + LAG)
 
 GATHERS = [(0, 768), (768, 1408), (1408, 2048)]
@@ -164,10 +164,8 @@ def tile_moe_bdx_glu_silu_kernel(
         def make_term(t):
             if t == 0:
                 term[t] = keep.tile([P, PACK, P], F32, name="first_term", tag="dy_w", align_bytes=64)
-            elif t == TILES - 1:
-                term[t] = keep.tile([P, PACK, P], F32, name="last_term")
             else:
-                term[t] = work.tile([P, PACK, P], F32, name="term", bufs=TERM_BUFFERS)
+                term[t] = work.tile([P, PACK, P], F32, name="term%d" % (t % 2), bufs=TERM_BUFFERS[t % 2])
             if t in REST_ON_GPSIMD:
                 rest[t] = term[t]
                 nc.gpsimd.tensor_scalar(out=rest[t][:], in0=silu[t][:], scalar1=-1.0, scalar2=1.0, op0=ALU.mult, op1=ALU.add)

@@ -40,8 +40,9 @@ REST_ON_GPSIMD = (PER_EXPERT + LAG, 2 * PER_EXPERT + LAG)
 
 GATHERS = [(0, 768), (768, 1408), (1408, 2048)]
 
-FIRST_PIECE = 512
-STORES = [(0, 384), (384, 704), (704, 896), (896, 1024)]
+OWN = (160, 320)
+RANGES = [(0, 160), OWN, (320, 512), (512, 704), (704, 896), (896, 1024)]
+STORES = [(0, 320), (320, 704), (704, 896), (896, 1024)]
 
 
 def tile_moe_bdx_glu_silu_kernel(
@@ -200,12 +201,8 @@ def tile_moe_bdx_glu_silu_kernel(
         last = E - 1
         most = C - P
 
-        def column(e, a, j):
-            if e < last:
-                return a * C + j * P
-            if a == DA3:
-                return most + j * P
-            return j * P if j < PER_EXPERT - 1 else most + C
+        def column(a, j):
+            return a * C + j * P
 
         def last_product(t, a, first_slot=0, end_slot=P):
             e, j = divmod(t, PER_EXPERT)
@@ -214,7 +211,7 @@ def tile_moe_bdx_glu_silu_kernel(
                 codes[e] = work.tile([P, 2 * C], U32, name="codes", bufs=E, align_bytes=64)
                 scales[e] = work.tile([P, 2 * C], U8, name="scales", bufs=E, align_bytes=64)
             factor = saved(a1_sb, A1_LOADS, t) if a == DA3 else term[t][:]
-            lo = PACK * column(e, a, j)
+            lo = PACK * column(a, j)
             pairs = slice(first_slot // 2, end_slot // 2)
             nc.vector.tensor_tensor(
                 out=grouped[e][:, lo : lo + PACK * P].rearrange("p (pair two d) -> p pair d two", d=PACK, two=2)[:, pairs],
@@ -228,20 +225,20 @@ def tile_moe_bdx_glu_silu_kernel(
                 out=codes[e][:, lo:hi].bitcast(E5M2X4), scales=scales[e][:, lo:hi], in_=grouped[e][:, PACK * lo : PACK * hi]
             )
 
-        def second_pass(acc, e, a, lo, first_pass):
+        def second_pass(acc, e, a, lo, hi):
             nc.tensor.matmul_mx(
-                out=acc[:],
+                out=acc[:, lo:hi],
                 lhsT=w13_w_view[:, a, e, :].bitcast(E2M1X4),
                 lhsT_scale=w13_s_view[:, a, e, :],
-                rhs=codes[e][:, lo : lo + C].bitcast(E5M2X4),
-                rhs_scale=scales[e][:, lo : lo + C],
-                start=first_pass,
-                stop=not first_pass,
+                rhs=codes[e][:, a * C + lo : a * C + hi].bitcast(E5M2X4),
+                rhs_scale=scales[e][:, a * C + lo : a * C + hi],
+                start=a == DA3,
+                stop=a == DA1,
             )
 
         def second_product(e, acc):
-            second_pass(acc, e, DA3, DA3 * C, True)
-            second_pass(acc, e, DA1, DA1 * C, False)
+            second_pass(acc, e, DA3, 0, C)
+            second_pass(acc, e, DA1, 0, C)
             nc.scalar.copy(out=dx[:, e * C : (e + 1) * C], in_=acc[:])
 
         for step in range(-TANH_LEAD, TILES):
@@ -263,12 +260,12 @@ def tile_moe_bdx_glu_silu_kernel(
             if whole_experts >= 1 and place == 0:
                 quantize(whole_experts - 1, 0, 2 * C)
 
-        final_da1 = column(last, DA1, PER_EXPERT - 1)
+        final_da1 = column(DA1, PER_EXPERT - 1)
         last_product(TILES - 2, DA3)
         last_product(TILES - 2, DA1)
         last_product(TILES - 1, DA3)
         quantize(last, 0, 2 * P)
-        quantize(last, most, most + C)
+        quantize(last, C, 2 * C)
         quantize(last, 2 * P, most)
         last_product(TILES - 1, DA1, 0, P // 2)
         last_product(TILES - 1, DA1, P // 2, P)
@@ -280,18 +277,26 @@ def tile_moe_bdx_glu_silu_kernel(
         second_product(2, spare)
 
         early, final = turns
-        second_pass(final, last, DA3, most, True)
-        second_pass(early, last, DA3, most, True)
-        second_pass(early, last, DA1, 0, False)
+        second_pass(final, last, DA3, most, C)
+        for lo, hi in ((0, 2 * P), (2 * P, most)):
+            second_pass(early, last, DA3, lo, hi)
+            second_pass(early, last, DA1, lo, hi)
         nc.scalar.copy(out=dx[:, last * C : last * C + most], in_=early[:, 0:most])
-        second_pass(final, last, DA1, final_da1 - most, False)
+        second_pass(final, last, DA1, most, C)
         nc.vector.tensor_copy(out=dx[:, last * C + most : E * C], in_=final[:, most:C])
 
         first = keep.tile([P, T], F32, name="first")
         total = keep.tile([P, T], F32, name="total")
-        for lo in range(0, T, FIRST_PIECE):
-            hi = lo + FIRST_PIECE
-            nc.vector.tensor_copy(first[:, lo:hi], dx[:].indirect(pos1_sb[:, lo // 16 : hi // 16]))
-        for lo, hi in STORES:
-            nc.vector.tensor_tensor(total[:, lo:hi], dx[:].indirect(pos2_sb[:, lo // 16 : hi // 16]), first[:, lo:hi], ALU.add)
-            nc.sync.dma_start(out=out[:, lo:hi], in_=total[:, lo:hi])
+
+        def picked(positions, lo, hi):
+            return dx[:].indirect(positions[:, lo // 16 : hi // 16])
+
+        nc.vector.tensor_copy(first[:, OWN[0] : OWN[1]], picked(pos1_sb, *OWN))
+        for lo, hi in RANGES:
+            if (lo, hi) != OWN:
+                nc.scalar.activation(out=first[:, lo:hi], in_=picked(pos1_sb, lo, hi), func=ACT.Copy)
+        for lo, hi in RANGES:
+            nc.vector.tensor_tensor(total[:, lo:hi], picked(pos2_sb, lo, hi), first[:, lo:hi], ALU.add)
+            for store_lo, store_hi in STORES:
+                if store_hi == hi:
+                    nc.sync.dma_start(out=out[:, store_lo:store_hi], in_=total[:, store_lo:store_hi])

@@ -32,7 +32,7 @@ SILU_LEAD = 2
 TERM_LEAD = 1
 LAG = 2
 
-SUM_BANKS = 5
+SUM_BANKS = 6
 TURN_BANKS = 2
 
 TERM_BUFFERS = (1, 2)
@@ -136,9 +136,9 @@ def tile_moe_bdx_glu_silu_kernel(
         for lo, hi in GATHERS:
             nc.vector.tensor_copy(g_w[:, lo:hi], dy_w[:].bitcast(U32).indirect(offs_sb[:, lo // 16 : hi // 16]))
 
-        spare = psum.tile([P, C], F32, name="spare")
-        nc.tensor.transpose(spare[:, 0:P], gate_rows[:], ident[:])
-        nc.scalar.activation(out=half_gate[:], in_=spare[:, 0:TILES], func=ACT.Copy, scale=0.5)
+        gate_bank = sums[SUM_BANKS - 1]
+        nc.tensor.transpose(gate_bank[:, 0:P], gate_rows[:], ident[:])
+        nc.scalar.activation(out=half_gate[:], in_=gate_bank[:, 0:TILES], func=ACT.Copy, scale=0.5)
 
         tanh, gated, silu, rest, term = {}, {}, {}, {}, {}
 
@@ -274,7 +274,7 @@ def tile_moe_bdx_glu_silu_kernel(
 
         second_product(0, sums[(TILES - 3) % SUM_BANKS])
         second_product(1, sums[(TILES - 2) % SUM_BANKS])
-        second_product(2, spare)
+        second_product(2, sums[(TILES - 4) % SUM_BANKS])
 
         early, final = turns
         second_pass(final, last, DA3, most, C)

from contextlib import ExitStack

import concourse.mybir as mybir
from concourse.masks import make_identity

K, T, E, C, H, N = 128, 1024, 4, 512, 512, 512
FLOPS = 2 * E * C * (N * H + 2 * H * K)
BYTES = T * N + T * 16 + 2 * 4 * H * E * C + E * (N * H + 2 * H * K) // 2 + E * 16 * (H + 2 * K) + 4 * E * C + 2 * 128 * 256 + 4 * K * T

F32 = mybir.dt.float32
BF16 = mybir.dt.bfloat16
I32 = mybir.dt.int32
U32 = mybir.dt.uint32
U16 = mybir.dt.uint16
U8 = mybir.dt.uint8
E5M2X4 = mybir.dt.float8_e5m2_x4
E2M1X4 = mybir.dt.float4_e2m1fn_x4
ACT = mybir.ActivationFunctionType
ALU = mybir.AluOpType

P = 128
PACK = 4
TILES = E * C // P
PER_EXPERT = C // P
DA1, DA3 = 0, 1

A1_LOADS = [(0, 128), (128, 384), (384, 768), (768, 1024), (1024, 1536), (1536, 2048)]
A3_LOADS = [(0, 256), (256, 512), (512, 1024), (1024, 1536), (1536, 2048)]

TANH_LEAD = 3
SILU_LEAD = 2
TERM_LEAD = 1
LAG = 2

SUM_BANKS = 6
TURN_BANKS = 2

TERM_BUFFERS = (1, 2)
REST_ON_GPSIMD = (PER_EXPERT + LAG, 2 * PER_EXPERT + LAG)

GATHERS = [(0, 768), (768, 1408), (1408, 2048)]

OWN = (160, 320)
RANGES = [(0, 160), OWN, (320, 512), (512, 704), (704, 896), (896, 1024)]
STORES = [(0, 320), (320, 704), (704, 896), (896, 1024)]


def tile_moe_bdx_glu_silu_kernel(
    tc, dy_words, dy_scales, a1, a3, w2_words, w2_scales, w1_words, w1_scales, w3_words, w3_scales,
    gate, offs, pos1, pos2, out,
):
    nc = tc.nc
    with ExitStack() as ctx:
        keep = ctx.enter_context(tc.tile_pool(name="keep", bufs=1))
        work = ctx.enter_context(tc.tile_pool(name="work", bufs=3))
        psum = ctx.enter_context(tc.psum_pool(name="psum", bufs=1))

        offs_sb = keep.tile([P, E * C // 16], U16, name="offs_sb")
        pos1_sb = keep.tile([P, T // 16], U16, name="pos1_sb")
        pos2_sb = keep.tile([P, T // 16], U16, name="pos2_sb")
        dy_w = keep.tile([P, T], I32, name="dy_w", align_bytes=64)
        dy_s = keep.tile([P, T], U8, name="dy_s", align_bytes=64)
        w2_w = keep.tile([P, E * 2 * H], U8, name="w2_w", align_bytes=64)
        w2_s = keep.tile([P, E * H], U8, name="w2_s", align_bytes=64)
        w13_w = keep.tile([P, 2 * E * 2 * K], U8, name="w13_w", align_bytes=64)
        w13_s = keep.tile([P, 2 * E * K], U8, name="w13_s", align_bytes=64)
        gate_rows = keep.tile([P, P], F32, name="gate_rows")
        half_gate = keep.tile([P, TILES], F32, name="half_gate")
        ident = keep.tile([P, P], F32, name="ident")
        dx = keep.tile([P, E * C], F32, name="dx")
        a1_sb = [keep.tile([P, PACK, hi - lo], F32, name="a1_sb%d" % lo) for lo, hi in A1_LOADS]
        a3_sb = [keep.tile([P, PACK, hi - lo], F32, name="a3_sb%d" % lo) for lo, hi in A3_LOADS]
        g_w = keep.tile([P, E * C], U32, name="g_w", align_bytes=64)
        g_s = keep.tile([P, E * C], U8, name="g_s", align_bytes=64)
        sums = [psum.tile([P, H], F32, name="sums%d" % b) for b in range(SUM_BANKS)]
        turns = [psum.tile([P, H], F32, name="turns%d" % b) for b in range(TURN_BANKS)]

        nc.gpsimd.memset(dy_s[:].bitcast(I32), 0)
        for plane in (w2_s, w13_s):
            nc.vector.memset(plane[:].bitcast(I32), 0)
        nc.gpsimd.memset(gate_rows[:], 0.0)
        make_identity(nc, ident[:])

        def load_scales(plane_view, rows):
            for q in range(4):
                nc.sync.dma_start(out=plane_view[32 * q : 32 * q + 4].bitcast(I32), in_=rows[4 * q : 4 * q + 4].bitcast(I32))

        def load_a1(c):
            lo, hi = A1_LOADS[c]
            nc.sync.dma_start(out=a1_sb[c][:], in_=a1[:, lo:hi].rearrange("(p d) s -> p d s", d=PACK))

        def load_a3(c):
            lo, hi = A3_LOADS[c]
            nc.sync.dma_start(out=a3_sb[c][:], in_=a3[:, lo:hi].rearrange("(p d) s -> p d s", d=PACK))

        def load_w2(first_expert, end_expert):
            nc.sync.dma_start(
                out=w2_w[:].rearrange("p (e c) -> p e c", e=E)[:, first_expert:end_expert].bitcast(I32),
                in_=w2_words.rearrange("e s p c -> p (e s) c")[:, first_expert:end_expert].bitcast(I32),
            )

        def saved(tiles, loads, t):
            c = max(n for n, (lo, hi) in enumerate(loads) if lo <= t * P)
            lo = t * P - loads[c][0]
            return tiles[c][:, :, lo : lo + P]

        w13_w_view = w13_w[:].rearrange("p (a e c) -> p a e c", a=2, e=E)
        w13_s_view = w13_s[:].rearrange("p (a e c) -> p a e c", a=2, e=E)
        nc.sync.dma_start(offs_sb[:], offs)
        load_scales(dy_s[:], dy_scales[0])
        load_a1(0)
        nc.sync.dma_start(out=gate_rows[0:TILES, :], in_=gate[0].rearrange("(t s) -> t s", s=P))
        load_a1(1)
        nc.sync.dma_start(out=dy_w[:], in_=dy_words[0].rearrange("p t d -> p (t d)").bitcast(I32))
        load_a1(2)
        load_scales(w2_s[:].rearrange("p (e c) -> p e c", e=E), w2_scales.rearrange("e s f c -> f (e s) c"))
        load_w2(0, E // 2)
        load_a3(0)
        load_a1(3)
        load_a3(1)
        load_a3(2)
        load_w2(E // 2, E)
        load_a1(4)
        load_a3(3)
        load_a1(5)
        load_a3(4)
        for a, weight_scales in ((DA1, w1_scales), (DA3, w3_scales)):
            load_scales(w13_s_view[:, a], weight_scales.rearrange("e s f c -> f (e s) c"))
        for a, weight_words in ((DA1, w1_words), (DA3, w3_words)):
            nc.sync.dma_start(out=w13_w_view[:, a].bitcast(I32), in_=weight_words.rearrange("e s p c -> p (e s) c").bitcast(I32))
        nc.sync.dma_start(pos1_sb[:], pos1)
        nc.sync.dma_start(pos2_sb[:], pos2)

        for lo, hi in GATHERS:
            nc.vector.tensor_copy(g_s[:, lo:hi], dy_s[:].indirect(offs_sb[:, lo // 16 : hi // 16]))
        for lo, hi in GATHERS:
            nc.vector.tensor_copy(g_w[:, lo:hi], dy_w[:].bitcast(U32).indirect(offs_sb[:, lo // 16 : hi // 16]))

        gate_bank = sums[SUM_BANKS - 1]
        nc.tensor.transpose(gate_bank[:, 0:P], gate_rows[:], ident[:])
        nc.scalar.activation(out=half_gate[:], in_=gate_bank[:, 0:TILES], func=ACT.Copy, scale=0.5)

        tanh, gated, silu, rest, term = {}, {}, {}, {}, {}

        def make_tanh(t):
            bank = turns[t % TURN_BANKS]
            v = saved(a1_sb, A1_LOADS, t)
            for d in range(PACK):
                nc.tensor.transpose(bank[:, d * P : (d + 1) * P], v[:, d, :], ident[:])
            tanh[t] = work.tile([P, H], F32, name="tanh", bufs=4)
            nc.scalar.activation(out=tanh[t][:], in_=bank[:], func=ACT.Tanh, scale=0.5)

        def make_gated(t):
            gated[t] = work.tile([P, H], F32, name="gated", bufs=6)
            factor = half_gate[:, t : t + 1]
            nc.scalar.activation(out=gated[t][:], in_=tanh[t][:], func=ACT.Identity, scale=factor, bias=factor)

        def make_silu(t):
            silu[t] = work.tile([P, PACK, P], F32, name="silu", bufs=4)
            nc.scalar.activation(out=silu[t][:], in_=saved(a1_sb, A1_LOADS, t), func=ACT.Silu, scale=-1.0)
            if t not in REST_ON_GPSIMD:
                rest[t] = work.tile([P, PACK, P], F32, name="rest", bufs=5)
                nc.scalar.activation(out=rest[t][:], in_=silu[t][:], func=ACT.Copy, scale=-1.0, bias=1.0)

        def make_term(t):
            if t == 0:
                term[t] = keep.tile([P, PACK, P], F32, name="first_term", tag="dy_w", align_bytes=64)
            else:
                term[t] = work.tile([P, PACK, P], F32, name="term%d" % (t % 2), bufs=TERM_BUFFERS[t % 2])
            if t in REST_ON_GPSIMD:
                rest[t] = term[t]
                nc.gpsimd.tensor_scalar(out=rest[t][:], in0=silu[t][:], scalar1=-1.0, scalar2=1.0, op0=ALU.mult, op1=ALU.add)
            nc.gpsimd.tensor_tensor(out=term[t][:], in0=rest[t][:], in1=saved(a3_sb, A3_LOADS, t), op=ALU.mult)

        def first_product(t):
            e = t // PER_EXPERT
            slots = slice(t * P, (t + 1) * P)
            nc.tensor.matmul_mx(
                out=sums[t % SUM_BANKS][:],
                lhsT=g_w[:, slots].bitcast(E5M2X4),
                lhsT_scale=g_s[:, slots],
                rhs=w2_w[:, e * 2 * H : (e + 1) * 2 * H].bitcast(E2M1X4),
                rhs_scale=w2_s[:, e * H : (e + 1) * H],
                start=True,
                stop=True,
            )

        def make_common(t):
            bank = sums[t % SUM_BANKS]
            common = work.tile([P, PACK, P], F32, name="common", bufs=3)
            nc.vector.tensor_tensor(
                out=common[:],
                in0=bank[:].rearrange("s (p d) -> s d p", d=PACK),
                in1=gated[t][:].rearrange("s (d p) -> s d p", d=PACK),
                op=ALU.mult,
            )
            for d in range(PACK):
                nc.tensor.transpose(bank[:, d * P : (d + 1) * P], common[:, d, :], ident[:])

        grouped, codes, scales = {}, {}, {}
        last = E - 1
        most = C - P

        def column(a, j):
            return a * C + j * P

        def last_product(t, a, first_slot=0, end_slot=P):
            e, j = divmod(t, PER_EXPERT)
            if e not in grouped:
                grouped[e] = work.tile([P, 2 * C * PACK], BF16, name="grouped", bufs=E, align_bytes=64)
                codes[e] = work.tile([P, 2 * C], U32, name="codes", bufs=E, align_bytes=64)
                scales[e] = work.tile([P, 2 * C], U8, name="scales", bufs=E, align_bytes=64)
            factor = saved(a1_sb, A1_LOADS, t) if a == DA3 else term[t][:]
            lo = PACK * column(a, j)
            pairs = slice(first_slot // 2, end_slot // 2)
            nc.vector.tensor_tensor(
                out=grouped[e][:, lo : lo + PACK * P].rearrange("p (pair two d) -> p pair d two", d=PACK, two=2)[:, pairs],
                in0=sums[t % SUM_BANKS][:].rearrange("p (d pair two) -> p pair d two", d=PACK, two=2)[:, pairs],
                in1=factor.rearrange("p d (pair two) -> p pair d two", two=2)[:, pairs],
                op=ALU.mult,
            )

        def quantize(e, lo, hi):
            nc.vector.quantize_mx(
                out=codes[e][:, lo:hi].bitcast(E5M2X4), scales=scales[e][:, lo:hi], in_=grouped[e][:, PACK * lo : PACK * hi]
            )

        def second_pass(acc, e, a, lo, hi):
            nc.tensor.matmul_mx(
                out=acc[:, lo:hi],
                lhsT=w13_w_view[:, a, e, :].bitcast(E2M1X4),
                lhsT_scale=w13_s_view[:, a, e, :],
                rhs=codes[e][:, a * C + lo : a * C + hi].bitcast(E5M2X4),
                rhs_scale=scales[e][:, a * C + lo : a * C + hi],
                start=a == DA3,
                stop=a == DA1,
            )

        def second_product(e, acc):
            second_pass(acc, e, DA3, 0, C)
            second_pass(acc, e, DA1, 0, C)
            nc.scalar.copy(out=dx[:, e * C : (e + 1) * C], in_=acc[:])

        for step in range(-TANH_LEAD, TILES):
            if step + TANH_LEAD < TILES:
                make_tanh(step + TANH_LEAD)
                make_gated(step + TANH_LEAD)
            if 0 <= step + SILU_LEAD < TILES:
                make_silu(step + SILU_LEAD)
            if 0 <= step + TERM_LEAD < TILES:
                make_term(step + TERM_LEAD)
            if 0 <= step + 1 < TILES:
                first_product(step + 1)
            if 0 <= step:
                make_common(step)
            if 0 <= step - LAG:
                last_product(step - LAG, DA3)
                last_product(step - LAG, DA1)
            whole_experts, place = divmod(step - LAG, PER_EXPERT)
            if whole_experts >= 1 and place == 0:
                quantize(whole_experts - 1, 0, 2 * C)

        final_da1 = column(DA1, PER_EXPERT - 1)
        last_product(TILES - 2, DA3)
        last_product(TILES - 2, DA1)
        last_product(TILES - 1, DA3)
        quantize(last, 0, 2 * P)
        quantize(last, C, 2 * C)
        quantize(last, 2 * P, most)
        last_product(TILES - 1, DA1, 0, P // 2)
        last_product(TILES - 1, DA1, P // 2, P)
        quantize(last, final_da1, final_da1 + P // 2)
        quantize(last, final_da1 + P // 2, final_da1 + P)

        second_product(0, sums[(TILES - 3) % SUM_BANKS])
        second_product(1, sums[(TILES - 2) % SUM_BANKS])
        second_product(2, sums[(TILES - 4) % SUM_BANKS])

        early, final = turns
        second_pass(final, last, DA3, most, C)
        for lo, hi in ((0, 2 * P), (2 * P, most)):
            second_pass(early, last, DA3, lo, hi)
            second_pass(early, last, DA1, lo, hi)
        nc.scalar.copy(out=dx[:, last * C : last * C + most], in_=early[:, 0:most])
        second_pass(final, last, DA1, most, C)
        nc.vector.tensor_copy(out=dx[:, last * C + most : E * C], in_=final[:, most:C])

        first = keep.tile([P, T], F32, name="first")
        total = keep.tile([P, T], F32, name="total")

        def picked(positions, lo, hi):
            return dx[:].indirect(positions[:, lo // 16 : hi // 16])

        nc.vector.tensor_copy(first[:, OWN[0] : OWN[1]], picked(pos1_sb, *OWN))
        for lo, hi in RANGES:
            if (lo, hi) != OWN:
                nc.scalar.activation(out=first[:, lo:hi], in_=picked(pos1_sb, lo, hi), func=ACT.Copy)
        for lo, hi in RANGES:
            nc.vector.tensor_tensor(total[:, lo:hi], picked(pos2_sb, lo, hi), first[:, lo:hi], ALU.add)
            for store_lo, store_hi in STORES:
                if store_hi == hi:
                    nc.sync.dma_start(out=out[:, store_lo:store_hi], in_=total[:, store_lo:store_hi])
